import numpy as np
import ml_dtypes


def mxq(x, axis, fmt="e4m3"):
    dtype, down = {"e4m3": (ml_dtypes.float8_e4m3fn, 7), "e5m2": (ml_dtypes.float8_e5m2, 14)}[fmt]
    v = np.moveaxis(np.asarray(x, np.float32).astype(ml_dtypes.bfloat16).astype(np.float64), axis, -1)
    blocks = v.reshape(v.shape[:-1] + (-1, 32))
    amax = np.abs(blocks).max(-1, keepdims=True)
    byte = np.maximum(np.where(amax > 0, np.frexp(amax)[1] - 1 + 127, 0) - down, 1)
    scale = np.exp2(byte - 127.0)
    codes = (blocks / scale).astype(np.float32).astype(dtype).astype(np.float64)
    return np.moveaxis((codes * scale).reshape(v.shape), -1, axis)


WIDE = False


def mx_kscale(k):
    if not WIDE:
        return np.ones(k)
    levels = np.array([10, -10, 5, -5, 0])
    if k % 512:
        return np.exp2(np.random.permutation(np.resize(levels, k // 32))).repeat(32)
    a = np.empty((k // 512, 16))
    for p in range(k // 512):
        a[p, :8] = np.random.permutation(np.resize(levels, 8))
        for g in range(8):
            far = levels[np.abs(levels - a[p, g]) >= 10]
            a[p, g + 8] = far[np.random.randint(len(far))]
    return np.exp2(a.ravel()).repeat(32)


def f64(x):
    return np.asarray(x).astype(np.float64)


def striped(idx):
    return np.tile(idx.reshape(-1, 16).T, (8, 1)).astype(np.uint16)


def unstriped(offs):
    return offs[:16].T.reshape(-1).astype(np.int64)


E2M1 = np.array([0.0, 0.5, 1.0, 1.5, 2.0, 3.0, 4.0, 6.0, -0.0, -0.5, -1.0, -1.5, -2.0, -3.0, -4.0, -6.0])


def pack_weight(w, fmt):
    k, n = w.shape
    w = f64(np.asarray(w, np.float32).astype(ml_dtypes.bfloat16)).reshape(k // 32, 32, n)
    amax = np.abs(w).max(1)
    if fmt == "e4m3":
        byte = np.frexp(amax)[1] - 1 + 127 - 7
    else:
        mant, ex = np.frexp(amax / 6.0)
        byte = np.where(mant > 0.5, ex, ex - 1) + 127
    byte = np.clip(np.where(amax > 0, byte, 1), 1, 254)
    scaled = (w * np.exp2(127.0 - byte)[:, None, :]).reshape(k, n).astype(np.float32)
    by_word = np.ascontiguousarray(scaled.reshape(k // 512, 128, 4, n).transpose(0, 1, 3, 2))
    if fmt == "e4m3":
        words = by_word.astype(ml_dtypes.float8_e4m3fn).view(np.uint8)
    else:
        c = by_word.astype(ml_dtypes.float4_e2m1fn).view(np.uint8) & 0xF
        words = (c[..., 0::2] | (c[..., 1::2] << 4)).reshape(k // 512, 128, 2 * n)
    return np.ascontiguousarray(words), np.ascontiguousarray(byte.astype(np.uint8).reshape(k // 512, 16, n))


def unpack_weight(words, scales, fmt):
    g, _, n = scales.shape
    words = np.ascontiguousarray(words).reshape(g, 128, n, -1)
    if fmt == "e4m3":
        vals = words.view(ml_dtypes.float8_e4m3fn).astype(np.float64)
    else:
        nib = np.empty((g, 128, n, 4), np.uint8)
        nib[..., 0::2] = words & 0xF
        nib[..., 1::2] = words >> 4
        vals = E2M1[nib]
    vals = vals * np.repeat(np.exp2(scales.astype(np.float64) - 127.0), 8, axis=1)[..., None]
    return vals.transpose(0, 1, 3, 2).reshape(g * 512, n)


K, T, E, C, N = 1024, 768, 6, 128, 128
M = 512


def by_expert(wq, xq):
    return np.concatenate([wq[e].T @ xq[:, e * C:(e + 1) * C] for e in range(E)], axis=1)


def setup_inputs():
    n = np.random.standard_normal
    s = mx_kscale(K)[:, None]
    w = [pack_weight(m, "e2m1") for m in n((E, K, N)) / np.sqrt(K) / s[None]]
    r = mx_kscale(M)[:, None]
    return {
        "uT": (n((M, T)) * r).astype(np.float32),
        "wu": (n((M, K)) / np.sqrt(M) / r * s.T).astype(np.float32),
        "w_words": np.stack([m[0] for m in w]),
        "w_scales": np.stack([m[1] for m in w]),
        "gate": np.tile(np.random.uniform(0.2, 1.0, E * C), (N, 1)).astype(np.float32),
        "offs": striped(np.random.permutation(T)[:E * C]),
    }


def reference(uT, wu, w_words, w_scales, gate, offs):
    idx = unstriped(offs)
    w = np.stack([unpack_weight(w_words[e], w_scales[e], "e2m1") for e in range(E)])
    x = mxq(f64(wu), 0, "e4m3").T @ mxq(f64(uT), 0, "e4m3")
    xq = mxq(x[:, idx], 0, "e4m3")
    y = by_expert(w, xq)
    out = np.zeros((N, T))
    out[:, idx] = f64(gate) * y
    return out

@@ -1,0 +1,169 @@
+from contextlib import ExitStack
+
+import concourse.mybir as mybir
+
+K, T, E, C, N, M = 1024, 768, 6, 128, 128, 512
+FLOPS = 2 * M * K * T + 2 * K * N * T
+
+F32 = mybir.dt.float32
+BF16 = mybir.dt.bfloat16
+I32 = mybir.dt.int32
+U32 = mybir.dt.uint32
+U16 = mybir.dt.uint16
+U8 = mybir.dt.uint8
+FP8X4 = mybir.dt.float8_e4m3fn_x4
+FP4X4 = mybir.dt.float4_e2m1fn_x4
+MULT = mybir.AluOpType.mult
+
+P = 128
+G = K // 512
+GROUP = 256
+GROUPS = T // GROUP
+
+
+def tile_moe_prv_lin_none_kernel(tc, uT, wu, w_words, w_scales, gate, offs, out):
+    nc = tc.nc
+    with ExitStack() as ctx:
+        keep = ctx.enter_context(tc.tile_pool(name="keep", bufs=1))
+        x_banks = ctx.enter_context(tc.psum_pool(name="x_banks", bufs=6))
+        y_banks = ctx.enter_context(tc.psum_pool(name="y_banks", bufs=2))
+
+        offsets = keep.tile([P, T // 16], U16, name="offsets")
+        u_raw = [keep.tile([P, 2, T], F32, name="u_raw%d" % h) for h in range(2)]
+        wu_raw = [[keep.tile([P, 4, 256], F32, name="wu_raw%d%d" % (g, h)) for h in range(2)] for g in range(G)]
+        words = keep.tile([P, E * G, 2 * N], U8, name="words", align_bytes=64)
+        word_scales = keep.tile([P, E * G, N], U8, name="word_scales", align_bytes=64)
+        gates = keep.tile([P, T], F32, name="gates")
+
+        nc.gpsimd.memset(word_scales[:].bitcast(I32), 0)
+
+        u_rows = uT.rearrange("(p j) t -> p j t", j=4)
+        wu_rows = wu.rearrange("(p j) k -> p j k", j=4)
+        nc.sync.dma_start(u_raw[0][:], u_rows[:, 0:2, :])
+        nc.sync.dma_start(offsets[:], offs)
+        nc.sync.dma_start(u_raw[1][:], u_rows[:, 2:4, :])
+        for g in range(G):
+            for h in range(2):
+                k0 = 512 * g + 256 * h
+                nc.sync.dma_start(wu_raw[g][h][:], wu_rows[:, :, k0 : k0 + 256])
+        scale_rows = w_scales.rearrange("e a q n -> q (e a) n").bitcast(I32)
+        for quad in range(4):
+            nc.sync.dma_start(
+                word_scales[32 * quad : 32 * quad + 4].bitcast(I32), scale_rows[4 * quad : 4 * quad + 4]
+            )
+        nc.sync.dma_start(words[:].bitcast(I32), w_words.rearrange("e a p n -> p (e a) n").bitcast(I32))
+        nc.sync.dma_start(gates[:], gate)
+
+        pairs = [keep.tile([P, 2 * T], BF16, name="pairs%d" % h) for h in range(2)]
+        u_slots = [keep.tile([P, 4 * GROUP], BF16, name="u_slots%d" % s, align_bytes=64) for s in range(GROUPS)]
+        u_codes = [keep.tile([P, GROUP], U32, name="u_codes%d" % s, align_bytes=64) for s in range(GROUPS)]
+        u_scales = [keep.tile([P, GROUP], U8, name="u_scales%d" % s, align_bytes=64) for s in range(GROUPS)]
+        wu_bf = [keep.tile([P, 2048], BF16, name="wu_bf%d" % g, align_bytes=64) for g in range(G)]
+        wu_codes = [keep.tile([P, 512], U32, name="wu_codes%d" % g, align_bytes=64) for g in range(G)]
+        wu_scales = [keep.tile([P, 512], U8, name="wu_scales%d" % g, align_bytes=64) for g in range(G)]
+        x_bf = [keep.tile([P, G * 4 * C], BF16, name="x_bf%d" % e, align_bytes=64) for e in range(E)]
+        x_codes = [keep.tile([P, G * C], U32, name="x_codes%d" % e, align_bytes=64) for e in range(E)]
+        x_scales = [keep.tile([P, G * C], U8, name="x_scales%d" % e, align_bytes=64) for e in range(E)]
+        gated = [keep.tile([P, C], F32, name="gated%d" % e) for e in range(E)]
+        by_token = keep.tile([P, T], F32, name="by_token")
+
+        def round_u(copy, h, t0, t1):
+            copy(
+                pairs[h][:].rearrange("p (t e) -> p t e", e=2)[:, t0:t1, :],
+                u_raw[h][:].rearrange("p e t -> p t e")[:, t0:t1, :],
+            )
+
+        def gather_u(h, s):
+            nc.vector.tensor_copy(
+                u_slots[s][:].bitcast(U32).rearrange("p (c h) -> p c h", h=2)[:, :, h],
+                pairs[h][:].bitcast(U32).indirect(offsets[:, s * GROUP // 16 : (s + 1) * GROUP // 16]),
+            )
+
+        def quantize(codes, scales, values):
+            nc.vector.quantize_mx(out=codes.bitcast(FP8X4), scales=scales, in_=values)
+
+        def round_wu(copy, g, h, m0, m1):
+            copy(
+                wu_bf[g][:].rearrange("p (t m j) -> p m t j", t=4, j=4)[:, 64 * h + m0 : 64 * h + m1],
+                wu_raw[g][h][:].rearrange("p j (m t) -> p m t j", t=4)[:, m0:m1],
+            )
+
+        def project(e, g, copy):
+            s, c0 = divmod(e * C, GROUP)
+            bank = x_banks.tile([P, 4, C], F32, name="x_bank")
+            for t in range(4):
+                nc.tensor.matmul_mx(
+                    out=bank[:, t, :],
+                    lhsT=wu_codes[g][:, t * P : (t + 1) * P].bitcast(FP8X4),
+                    lhsT_scale=wu_scales[g][:, t * P : (t + 1) * P],
+                    rhs=u_codes[s][:, c0 : c0 + C].bitcast(FP8X4),
+                    rhs_scale=u_scales[s][:, c0 : c0 + C],
+                    start=True,
+                    stop=True,
+                )
+            copy(
+                x_bf[e][:, g * 4 * C : (g + 1) * 4 * C].rearrange("p (c t) -> p c t", t=4),
+                bank[:].rearrange("p t c -> p c t"),
+            )
+
+        def quantize_x(e, g0, g1):
+            quantize(x_codes[e][:, g0 * C : g1 * C], x_scales[e][:, g0 * C : g1 * C], x_bf[e][:, g0 * 4 * C : g1 * 4 * C])
+
+        def expert(e):
+            bank = y_banks.tile([P, C], F32, name="y_bank")
+            for g in range(G):
+                nc.tensor.matmul_mx(
+                    out=bank[:],
+                    lhsT=words[:, e * G + g, :].bitcast(FP4X4),
+                    lhsT_scale=word_scales[:, e * G + g, :],
+                    rhs=x_codes[e][:, g * C : (g + 1) * C].bitcast(FP8X4),
+                    rhs_scale=x_scales[e][:, g * C : (g + 1) * C],
+                    start=(g == 0),
+                    stop=(g == G - 1),
+                )
+            nc.vector.tensor_tensor(gated[e][:], bank[:], gates[:, e * C : (e + 1) * C], MULT)
+
+        def scatter(e):
+            nc.vector.tensor_copy(by_token[:].indirect(offsets[:, e * C // 16 : (e + 1) * C // 16]), gated[e][:])
+
+        on_vector, on_scalar = nc.vector.tensor_copy, nc.scalar.copy
+
+        round_u(on_vector, 0, 0, 512)
+        round_u(on_scalar, 0, 512, T)
+        round_u(on_scalar, 1, 0, 512)
+        round_u(on_vector, 1, 512, T)
+        for s in range(GROUPS):
+            gather_u(0, s)
+        round_wu(on_scalar, 0, 0, 0, 64)
+        round_wu(on_scalar, 0, 1, 0, 64)
+        gather_u(1, 0)
+        gather_u(1, 1)
+        quantize(u_codes[0][:], u_scales[0][:], u_slots[0][:])
+        quantize(wu_codes[0][:], wu_scales[0][:], wu_bf[0][:])
+        gather_u(1, 2)
+        quantize(u_codes[1][:], u_scales[1][:], u_slots[1][:])
+        round_wu(on_scalar, 1, 0, 0, 64)
+        round_wu(on_vector, 1, 1, 0, 64)
+        quantize(u_codes[2][:], u_scales[2][:], u_slots[2][:])
+        quantize(wu_codes[1][:], wu_scales[1][:], wu_bf[1][:])
+
+        project(0, 0, on_scalar)
+        project(1, 0, on_scalar)
+        project(0, 1, on_scalar)
+        quantize_x(0, 0, G)
+        project(1, 1, on_scalar)
+        for e in range(E):
+            if e + 2 < E:
+                project(e + 2, 0, on_scalar)
+            if e + 1 < E - 1:
+                quantize_x(e + 1, 0, G)
+            elif e + 1 == E - 1:
+                quantize_x(e + 1, 0, 1)
+                quantize_x(e + 1, 1, G)
+            expert(e)
+            if e + 2 < E:
+                project(e + 2, 1, on_scalar)
+            if e > 0:
+                scatter(e - 1)
+        scatter(E - 1)
+        nc.sync.dma_start(out, by_token[:])

@@ -51,10 +51,13 @@ def tile_moe_prv_lin_none_kernel(tc, uT, wu, w_words, w_scales, gate, offs, out)
             nc.sync.dma_start(
                 word_scales[32 * quad : 32 * quad + 4].bitcast(I32), scale_rows[4 * quad : 4 * quad + 4]
             )
-        nc.sync.dma_start(words[:].bitcast(I32), w_words.rearrange("e a p n -> p (e a) n").bitcast(I32))
-        nc.sync.dma_start(gates[:], gate)
+        word_rows = w_words.rearrange("e a p n -> p (e a) n").bitcast(I32)
+        for h in range(2):
+            nc.sync.dma_start(words[:, E * h : E * (h + 1)].bitcast(I32), word_rows[:, E * h : E * (h + 1)])
+            nc.sync.dma_start(gates[:, h * T // 2 : (h + 1) * T // 2], gate[:, h * T // 2 : (h + 1) * T // 2])
 
         pairs = [keep.tile([P, 2 * T], BF16, name="pairs%d" % h) for h in range(2)]
+        u_planes = [keep.tile([P, 2, 2 * GROUP], BF16, name="u_planes%d" % s) for s in range(GROUPS)]
         u_slots = [keep.tile([P, 4 * GROUP], BF16, name="u_slots%d" % s, align_bytes=64) for s in range(GROUPS)]
         u_codes = [keep.tile([P, GROUP], U32, name="u_codes%d" % s, align_bytes=64) for s in range(GROUPS)]
         u_scales = [keep.tile([P, GROUP], U8, name="u_scales%d" % s, align_bytes=64) for s in range(GROUPS)]
@@ -64,7 +67,7 @@ def tile_moe_prv_lin_none_kernel(tc, uT, wu, w_words, w_scales, gate, offs, out)
         x_bf = [keep.tile([P, G * 4 * C], BF16, name="x_bf%d" % e, align_bytes=64) for e in range(E)]
         x_codes = [keep.tile([P, G * C], U32, name="x_codes%d" % e, align_bytes=64) for e in range(E)]
         x_scales = [keep.tile([P, G * C], U8, name="x_scales%d" % e, align_bytes=64) for e in range(E)]
-        gated = [keep.tile([P, C], F32, name="gated%d" % e) for e in range(E)]
+        by_slot = keep.tile([P, T], F32, name="by_slot")
         by_token = keep.tile([P, T], F32, name="by_token")
 
         def round_u(copy, h, t0, t1):
@@ -75,8 +78,14 @@ def tile_moe_prv_lin_none_kernel(tc, uT, wu, w_words, w_scales, gate, offs, out)
 
         def gather_u(h, s):
             nc.vector.tensor_copy(
-                u_slots[s][:].bitcast(U32).rearrange("p (c h) -> p c h", h=2)[:, :, h],
+                u_planes[s][:, h, :].bitcast(U32),
                 pairs[h][:].bitcast(U32).indirect(offsets[:, s * GROUP // 16 : (s + 1) * GROUP // 16]),
+            )
+
+        def interleave_u(s):
+            nc.vector.tensor_copy(
+                u_slots[s][:].rearrange("p (c h e) -> p c h e", h=2, e=2),
+                u_planes[s][:].rearrange("p h (c e) -> p c h e", e=2),
             )
 
         def quantize(codes, scales, values):
@@ -121,49 +130,54 @@ def tile_moe_prv_lin_none_kernel(tc, uT, wu, w_words, w_scales, gate, offs, out)
                     start=(g == 0),
                     stop=(g == G - 1),
                 )
-            nc.vector.tensor_tensor(gated[e][:], bank[:], gates[:, e * C : (e + 1) * C], MULT)
+            nc.scalar.copy(by_slot[:, e * C : (e + 1) * C], bank[:])
 
-        def scatter(e):
-            nc.vector.tensor_copy(by_token[:].indirect(offsets[:, e * C // 16 : (e + 1) * C // 16]), gated[e][:])
+        def scatter(e0, e1):
+            nc.vector.tensor_tensor(
+                by_token[:].indirect(offsets[:, e0 * C // 16 : e1 * C // 16]),
+                by_slot[:, e0 * C : e1 * C],
+                gates[:, e0 * C : e1 * C],
+                MULT,
+            )
 
         on_vector, on_scalar = nc.vector.tensor_copy, nc.scalar.copy
 
+        def slots(s):
+            gather_u(0, s)
+            gather_u(1, s)
+            interleave_u(s)
+            quantize(u_codes[s][:], u_scales[s][:], u_slots[s][:])
+
+        def round_wu_shared(g, h, m_vector):
+            if m_vector:
+                round_wu(on_vector, g, h, 0, m_vector)
+            round_wu(on_scalar, g, h, m_vector, 64)
+
         round_u(on_vector, 0, 0, 512)
         round_u(on_scalar, 0, 512, T)
-        round_u(on_scalar, 1, 0, 512)
-        round_u(on_vector, 1, 512, T)
-        for s in range(GROUPS):
-            gather_u(0, s)
-        round_wu(on_scalar, 0, 0, 0, 64)
-        round_wu(on_scalar, 0, 1, 0, 64)
-        gather_u(1, 0)
-        gather_u(1, 1)
-        quantize(u_codes[0][:], u_scales[0][:], u_slots[0][:])
+        round_u(on_vector, 1, 0, 256)
+        round_u(on_scalar, 1, 256, T)
+        slots(0)
+        round_wu_shared(0, 0, 0)
+        round_wu_shared(0, 1, 0)
         quantize(wu_codes[0][:], wu_scales[0][:], wu_bf[0][:])
-        gather_u(1, 2)
-        quantize(u_codes[1][:], u_scales[1][:], u_slots[1][:])
-        round_wu(on_scalar, 1, 0, 0, 64)
-        round_wu(on_vector, 1, 1, 0, 64)
-        quantize(u_codes[2][:], u_scales[2][:], u_slots[2][:])
+        round_wu_shared(1, 0, 0)
+        round_wu_shared(1, 1, 40)
         quantize(wu_codes[1][:], wu_scales[1][:], wu_bf[1][:])
-
         project(0, 0, on_scalar)
-        project(1, 0, on_scalar)
-        project(0, 1, on_scalar)
-        quantize_x(0, 0, G)
-        project(1, 1, on_scalar)
         for e in range(E):
-            if e + 2 < E:
-                project(e + 2, 0, on_scalar)
-            if e + 1 < E - 1:
-                quantize_x(e + 1, 0, G)
-            elif e + 1 == E - 1:
-                quantize_x(e + 1, 0, 1)
-                quantize_x(e + 1, 1, G)
+            project(e, 1, on_vector if e == 0 else on_scalar)
+            if e in (0, E - 1):
+                quantize_x(e, 0, 1)
+                quantize_x(e, 1, 2)
+            else:
+                quantize_x(e, 0, 2)
             expert(e)
-            if e + 2 < E:
-                project(e + 2, 1, on_scalar)
-            if e > 0:
-                scatter(e - 1)
-        scatter(E - 1)
+            if e + 1 < E:
+                if (e + 1) * C % GROUP == 0:
+                    slots((e + 1) * C // GROUP)
+                project(e + 1, 0, on_scalar)
+            if e >= 2:
+                scatter(e - 2, e - 1)
+        scatter(E - 2, E)
         nc.sync.dma_start(out, by_token[:])

@@ -17,20 +17,42 @@ MULT = mybir.AluOpType.mult
 
 P = 128
 G = K // 512
-GROUP = 256
-GROUPS = T // GROUP
+IL = "V"
+GROUPS = (4, 2)
+G0ONE = False
+U0V = 512
+U1V = 256
+WV = (0, 24, 0, 24)
+QXM = "m"
+SCM = (1, 1, 1, 1, 1, 1)
+LEAD = 1
+SCL = 2
+VEV = ((2, 0),)
+W0ONE = True
+W1ONE = False
+LATE = True
+ALIAS = ("il", 1)
+R = (3, 2)
+GSC = True
+WSPLIT = False
+OFFPOS = 1
 
 
 def tile_moe_prv_lin_none_kernel(tc, uT, wu, w_words, w_scales, gate, offs, out):
     nc = tc.nc
+    first = [sum(GROUPS[:s]) for s in range(len(GROUPS))]
+    group_of = [s for s, n in enumerate(GROUPS) for i in range(n)]
     with ExitStack() as ctx:
         keep = ctx.enter_context(tc.tile_pool(name="keep", bufs=1))
-        x_banks = ctx.enter_context(tc.psum_pool(name="x_banks", bufs=6))
-        y_banks = ctx.enter_context(tc.psum_pool(name="y_banks", bufs=2))
+        psum = ctx.enter_context(tc.psum_pool(name="psum", bufs=1))
 
         offsets = keep.tile([P, T // 16], U16, name="offsets")
         u_raw = [keep.tile([P, 2, T], F32, name="u_raw%d" % h) for h in range(2)]
-        wu_raw = [[keep.tile([P, 4, 256], F32, name="wu_raw%d%d" % (g, h)) for h in range(2)] for g in range(G)]
+        whole = (W0ONE, W1ONE)
+        pieces = [[(0, 128)] if whole[g] else [(0, 64), (64, 128)] for g in range(G)]
+        wu_raw = [
+            [keep.tile([P, 4, 4 * (m1 - m0)], F32, name="wu_raw%d%d" % (g, m0)) for m0, m1 in pieces[g]] for g in range(G)
+        ]
         words = keep.tile([P, E * G, 2 * N], U8, name="words", align_bytes=64)
         word_scales = keep.tile([P, E * G, N], U8, name="word_scales", align_bytes=64)
         gates = keep.tile([P, T], F32, name="gates")
@@ -39,29 +61,30 @@ def tile_moe_prv_lin_none_kernel(tc, uT, wu, w_words, w_scales, gate, offs, out)
 
         u_rows = uT.rearrange("(p j) t -> p j t", j=4)
         wu_rows = wu.rearrange("(p j) k -> p j k", j=4)
+        if OFFPOS == 0:
+            nc.sync.dma_start(offsets[:], offs)
         nc.sync.dma_start(u_raw[0][:], u_rows[:, 0:2, :])
-        nc.sync.dma_start(offsets[:], offs)
+        if OFFPOS == 1:
+            nc.sync.dma_start(offsets[:], offs)
         nc.sync.dma_start(u_raw[1][:], u_rows[:, 2:4, :])
         for g in range(G):
-            for h in range(2):
-                k0 = 512 * g + 256 * h
-                nc.sync.dma_start(wu_raw[g][h][:], wu_rows[:, :, k0 : k0 + 256])
+            for i, (m0, m1) in enumerate(pieces[g]):
+                nc.sync.dma_start(wu_raw[g][i][:], wu_rows[:, :, 512 * g + 4 * m0 : 512 * g + 4 * m1])
         scale_rows = w_scales.rearrange("e a q n -> q (e a) n").bitcast(I32)
         for quad in range(4):
-            nc.sync.dma_start(
+            (nc.gpsimd if GSC else nc.sync).dma_start(
                 word_scales[32 * quad : 32 * quad + 4].bitcast(I32), scale_rows[4 * quad : 4 * quad + 4]
             )
         word_rows = w_words.rearrange("e a p n -> p (e a) n").bitcast(I32)
-        for h in range(2):
-            nc.sync.dma_start(words[:, E * h : E * (h + 1)].bitcast(I32), word_rows[:, E * h : E * (h + 1)])
-            nc.sync.dma_start(gates[:, h * T // 2 : (h + 1) * T // 2], gate[:, h * T // 2 : (h + 1) * T // 2])
+        for e0, e1 in ((0, 3), (3, 6)) if WSPLIT else ((0, 6),):
+            nc.sync.dma_start(words[:, G * e0 : G * e1].bitcast(I32), word_rows[:, G * e0 : G * e1])
+            nc.sync.dma_start(gates[:, e0 * C : e1 * C], gate[:, e0 * C : e1 * C])
 
-        pairs = [keep.tile([P, 2 * T], BF16, name="pairs%d" % h) for h in range(2)]
-        u_planes = [keep.tile([P, 2, 2 * GROUP], BF16, name="u_planes%d" % s) for s in range(GROUPS)]
-        u_slots = [keep.tile([P, 4 * GROUP], BF16, name="u_slots%d" % s, align_bytes=64) for s in range(GROUPS)]
-        u_codes = [keep.tile([P, GROUP], U32, name="u_codes%d" % s, align_bytes=64) for s in range(GROUPS)]
-        u_scales = [keep.tile([P, GROUP], U8, name="u_scales%d" % s, align_bytes=64) for s in range(GROUPS)]
-        wu_bf = [keep.tile([P, 2048], BF16, name="wu_bf%d" % g, align_bytes=64) for g in range(G)]
+        pad = 256 if G0ONE else 0
+        pairs = [keep.tile([P, 2 * (T + (pad if h == 0 else 0))], BF16, name="pairs%d" % h) for h in range(2)]
+        u_codes = keep.tile([P, T], U32, name="u_codes", align_bytes=64)
+        u_scales = keep.tile([P, T], U8, name="u_scales", align_bytes=64)
+        wu_bf = [keep.tile([P, 2048], BF16, name="wu_bf%d" % g, tag="wu_bf%d" % g, align_bytes=64) for g in range(G)]
         wu_codes = [keep.tile([P, 512], U32, name="wu_codes%d" % g, align_bytes=64) for g in range(G)]
         wu_scales = [keep.tile([P, 512], U8, name="wu_scales%d" % g, align_bytes=64) for g in range(G)]
         x_bf = [keep.tile([P, G * 4 * C], BF16, name="x_bf%d" % e, align_bytes=64) for e in range(E)]
@@ -69,48 +92,87 @@ def tile_moe_prv_lin_none_kernel(tc, uT, wu, w_words, w_scales, gate, offs, out)
         x_scales = [keep.tile([P, G * C], U8, name="x_scales%d" % e, align_bytes=64) for e in range(E)]
         by_slot = keep.tile([P, T], F32, name="by_slot")
         by_token = keep.tile([P, T], F32, name="by_token")
+        all_planes = keep.tile([P, 2, 2 * T], BF16, name="all_planes")
+        all_slots = keep.tile([P, 4 * T], BF16, name="all_slots", align_bytes=64)
+        on_vector, on_scalar = nc.vector.tensor_copy, nc.scalar.copy
 
-        def round_u(copy, h, t0, t1):
-            copy(
-                pairs[h][:].rearrange("p (t e) -> p t e", e=2)[:, t0:t1, :],
-                u_raw[h][:].rearrange("p e t -> p t e")[:, t0:t1, :],
-            )
-
-        def gather_u(h, s):
-            nc.vector.tensor_copy(
-                u_planes[s][:, h, :].bitcast(U32),
-                pairs[h][:].bitcast(U32).indirect(offsets[:, s * GROUP // 16 : (s + 1) * GROUP // 16]),
-            )
-
-        def interleave_u(s):
-            nc.vector.tensor_copy(
-                u_slots[s][:].rearrange("p (c h e) -> p c h e", h=2, e=2),
-                u_planes[s][:].rearrange("p h (c e) -> p c h e", e=2),
-            )
+        def round_u(h, split):
+            for copy, t0, t1 in ((on_vector, 0, split), (on_scalar, split, T)):
+                if t1 > t0:
+                    copy(
+                        pairs[h][:].rearrange("p (t e) -> p t e", e=2)[:, t0:t1, :],
+                        u_raw[h][:].rearrange("p e t -> p t e")[:, t0:t1, :],
+                    )
 
         def quantize(codes, scales, values):
             nc.vector.quantize_mx(out=codes.bitcast(FP8X4), scales=scales, in_=values)
 
-        def round_wu(copy, g, h, m0, m1):
-            copy(
-                wu_bf[g][:].rearrange("p (t m j) -> p m t j", t=4, j=4)[:, 64 * h + m0 : 64 * h + m1],
-                wu_raw[g][h][:].rearrange("p j (m t) -> p m t j", t=4)[:, m0:m1],
-            )
+        def gather(h, c0, c1, planes, slot_major):
+            if IL == "step":
+                target = slot_major.bitcast(U32).rearrange("p (c h) -> p c h", h=2)[:, :, h]
+            else:
+                target = planes[:, h, :].bitcast(U32)
+            nc.vector.tensor_copy(target, pairs[h][:].bitcast(U32).indirect(offsets[:, c0 // 16 : c1 // 16]))
 
-        def project(e, g, copy):
-            s, c0 = divmod(e * C, GROUP)
-            bank = x_banks.tile([P, 4, C], F32, name="x_bank")
+        def slots(s):
+            c0, c1 = first[s] * C, (first[s] + GROUPS[s]) * C
+            planes = all_planes[:, :, 2 * c0 : 2 * c1]
+            slot_major = all_slots[:, 4 * c0 : 4 * c1]
+            if ALIAS == ("gg", s) and IL != "step":
+                own_planes = keep.tile([P, 2, 2 * (c1 - c0)], BF16, name="own_planes", tag="wu_bf1", align_bytes=64)
+                planes = own_planes[:]
+            elif ALIAS == ("il", s) or ALIAS == ("gg", s):
+                own_slots = keep.tile([P, 4 * (c1 - c0)], BF16, name="own_slots", tag="wu_bf1", align_bytes=64)
+                slot_major = own_slots[:]
+            if not G0ONE:
+                gather(0, c0, c1, planes, slot_major)
+            elif s == 0:
+                gather(0, 0, T, all_planes[:], all_slots[:])
+            gather(1, c0, c1, planes, slot_major)
+            if IL != "step":
+                (on_vector if IL == "V" else on_scalar)(
+                    slot_major.rearrange("p (c h e) -> p c h e", h=2, e=2),
+                    planes.rearrange("p h (c e) -> p c h e", e=2),
+                )
+            quantize(u_codes[:, c0:c1], u_scales[:, c0:c1], slot_major)
+
+        def weights(g):
+            for i, (m0, m1) in enumerate(pieces[g]):
+                split = WV[2 * g] + WV[2 * g + 1] if whole[g] else WV[2 * g + i]
+                for copy, a, b in ((on_vector, 0, split), (on_scalar, split, m1 - m0)):
+                    if b > a:
+                        copy(
+                            wu_bf[g][:].rearrange("p (t m j) -> p m t j", t=4, j=4)[:, m0 + a : m0 + b],
+                            wu_raw[g][i][:].rearrange("p j (m t) -> p m t j", t=4)[:, a:b],
+                        )
+            quantize(wu_codes[g][:], wu_scales[g][:], wu_bf[g][:])
+
+        ring, y_ring = R
+        uses = []
+        y_uses = []
+
+        def next_bank(shape, is_y):
+            if is_y and y_ring:
+                y_uses.append(0)
+                tag = "ybank%d" % ((len(y_uses) - 1) % y_ring)
+            else:
+                uses.append(0)
+                tag = "bank%d" % ((len(uses) - 1) % ring)
+            return psum.tile(shape, F32, name="bank", tag=tag)
+
+        def project(e, g):
+            bank = next_bank([P, 4, C], False)
             for t in range(4):
                 nc.tensor.matmul_mx(
                     out=bank[:, t, :],
                     lhsT=wu_codes[g][:, t * P : (t + 1) * P].bitcast(FP8X4),
                     lhsT_scale=wu_scales[g][:, t * P : (t + 1) * P],
-                    rhs=u_codes[s][:, c0 : c0 + C].bitcast(FP8X4),
-                    rhs_scale=u_scales[s][:, c0 : c0 + C],
+                    rhs=u_codes[:, e * C : (e + 1) * C].bitcast(FP8X4),
+                    rhs_scale=u_scales[:, e * C : (e + 1) * C],
                     start=True,
                     stop=True,
                 )
-            copy(
+            (on_vector if (e, g) in VEV else on_scalar)(
                 x_bf[e][:, g * 4 * C : (g + 1) * 4 * C].rearrange("p (c t) -> p c t", t=4),
                 bank[:].rearrange("p t c -> p c t"),
             )
@@ -119,7 +181,7 @@ def tile_moe_prv_lin_none_kernel(tc, uT, wu, w_words, w_scales, gate, offs, out)
             quantize(x_codes[e][:, g0 * C : g1 * C], x_scales[e][:, g0 * C : g1 * C], x_bf[e][:, g0 * 4 * C : g1 * 4 * C])
 
         def expert(e):
-            bank = y_banks.tile([P, C], F32, name="y_bank")
+            bank = next_bank([P, C], True)
             for g in range(G):
                 nc.tensor.matmul_mx(
                     out=bank[:],
@@ -132,52 +194,54 @@ def tile_moe_prv_lin_none_kernel(tc, uT, wu, w_words, w_scales, gate, offs, out)
                 )
             nc.scalar.copy(by_slot[:, e * C : (e + 1) * C], bank[:])
 
-        def scatter(e0, e1):
-            nc.vector.tensor_tensor(
-                by_token[:].indirect(offsets[:, e0 * C // 16 : e1 * C // 16]),
-                by_slot[:, e0 * C : e1 * C],
-                gates[:, e0 * C : e1 * C],
-                MULT,
-            )
+        ends = {sum(SCM[: i + 1]) - 1: sum(SCM[:i]) for i in range(len(SCM))}
 
-        on_vector, on_scalar = nc.vector.tensor_copy, nc.scalar.copy
+        def scatter(e):
+            if e in ends:
+                e0, e1 = ends[e], e + 1
+                nc.vector.tensor_tensor(
+                    by_token[:].indirect(offsets[:, e0 * C // 16 : e1 * C // 16]),
+                    by_slot[:, e0 * C : e1 * C],
+                    gates[:, e0 * C : e1 * C],
+                    MULT,
+                )
 
-        def slots(s):
-            gather_u(0, s)
-            gather_u(1, s)
-            interleave_u(s)
-            quantize(u_codes[s][:], u_scales[s][:], u_slots[s][:])
+        gathered = set()
+        projected = set()
 
-        def round_wu_shared(g, h, m_vector):
-            if m_vector:
-                round_wu(on_vector, g, h, 0, m_vector)
-            round_wu(on_scalar, g, h, m_vector, 64)
+        def need(e):
+            if group_of[e] not in gathered:
+                gathered.add(group_of[e])
+                slots(group_of[e])
 
-        round_u(on_vector, 0, 0, 512)
-        round_u(on_scalar, 0, 512, T)
-        round_u(on_vector, 1, 0, 256)
-        round_u(on_scalar, 1, 256, T)
-        slots(0)
-        round_wu_shared(0, 0, 0)
-        round_wu_shared(0, 1, 0)
-        quantize(wu_codes[0][:], wu_scales[0][:], wu_bf[0][:])
-        round_wu_shared(1, 0, 0)
-        round_wu_shared(1, 1, 40)
-        quantize(wu_codes[1][:], wu_scales[1][:], wu_bf[1][:])
-        project(0, 0, on_scalar)
+        def first_half(e):
+            if e < E and e not in projected:
+                projected.add(e)
+                need(e)
+                project(e, 0)
+
+        round_u(0, U0V)
+        round_u(1, U1V)
+        need(0)
+        weights(0)
+        if not LATE:
+            for e in range(E):
+                need(e)
+        weights(1)
+        for e in range(LEAD):
+            first_half(e)
         for e in range(E):
-            project(e, 1, on_vector if e == 0 else on_scalar)
-            if e in (0, E - 1):
+            first_half(e)
+            project(e, 1)
+            if QXM == "e" or (QXM == "m" and 0 < e < E - 1):
+                quantize_x(e, 0, 2)
+            else:
                 quantize_x(e, 0, 1)
                 quantize_x(e, 1, 2)
-            else:
-                quantize_x(e, 0, 2)
             expert(e)
-            if e + 1 < E:
-                if (e + 1) * C % GROUP == 0:
-                    slots((e + 1) * C // GROUP)
-                project(e + 1, 0, on_scalar)
-            if e >= 2:
-                scatter(e - 2, e - 1)
-        scatter(E - 2, E)
+            first_half(e + LEAD)
+            if e >= SCL:
+                scatter(e - SCL)
+        for e in range(E - SCL, E):
+            scatter(e)
         nc.sync.dma_start(out, by_token[:])

@@ -17,25 +17,27 @@ MULT = mybir.AluOpType.mult
 
 P = 128
 G = K // 512
-IL = "V"
+IL = "step"
 GROUPS = (4, 2)
 G0ONE = False
 U0V = 512
-U1V = 256
-WV = (0, 24, 0, 24)
-QXM = "m"
-SCM = (1, 1, 1, 1, 1, 1)
-LEAD = 1
-SCL = 2
-VEV = ((2, 0),)
-W0ONE = True
+U1V = 0
+WV = (0, 0, 0, 40)
+QXM = "g"
+SCM = (1, 1, 1, 1, 2)
+LEAD = 3
+SCL = 1
+VEV = ()
+W0ONE = False
 W1ONE = False
 LATE = True
-ALIAS = ("il", 1)
+ALIAS = None
 R = (3, 2)
 GSC = True
 WSPLIT = False
 OFFPOS = 1
+USPLIT = (False, True)
+UB = (256, 0)
 
 
 def tile_moe_prv_lin_none_kernel(tc, uT, wu, w_words, w_scales, gate, offs, out):
@@ -47,7 +49,8 @@ def tile_moe_prv_lin_none_kernel(tc, uT, wu, w_words, w_scales, gate, offs, out)
         psum = ctx.enter_context(tc.psum_pool(name="psum", bufs=1))
 
         offsets = keep.tile([P, T // 16], U16, name="offsets")
-        u_raw = [keep.tile([P, 2, T], F32, name="u_raw%d" % h) for h in range(2)]
+        u_cuts = [[(0, T // 2), (T // 2, T)] if USPLIT[h] else [(0, T)] for h in range(2)]
+        u_raw = [[keep.tile([P, 2, t1 - t0], F32, name="u_raw%d%d" % (h, t0)) for t0, t1 in u_cuts[h]] for h in range(2)]
         whole = (W0ONE, W1ONE)
         pieces = [[(0, 128)] if whole[g] else [(0, 64), (64, 128)] for g in range(G)]
         wu_raw = [
@@ -63,10 +66,12 @@ def tile_moe_prv_lin_none_kernel(tc, uT, wu, w_words, w_scales, gate, offs, out)
         wu_rows = wu.rearrange("(p j) k -> p j k", j=4)
         if OFFPOS == 0:
             nc.sync.dma_start(offsets[:], offs)
-        nc.sync.dma_start(u_raw[0][:], u_rows[:, 0:2, :])
+        for i, (t0, t1) in enumerate(u_cuts[0]):
+            nc.sync.dma_start(u_raw[0][i][:], u_rows[:, 0:2, t0:t1])
         if OFFPOS == 1:
             nc.sync.dma_start(offsets[:], offs)
-        nc.sync.dma_start(u_raw[1][:], u_rows[:, 2:4, :])
+        for i, (t0, t1) in enumerate(u_cuts[1]):
+            nc.sync.dma_start(u_raw[1][i][:], u_rows[:, 2:4, t0:t1])
         for g in range(G):
             for i, (m0, m1) in enumerate(pieces[g]):
                 nc.sync.dma_start(wu_raw[g][i][:], wu_rows[:, :, 512 * g + 4 * m0 : 512 * g + 4 * m1])
@@ -97,12 +102,14 @@ def tile_moe_prv_lin_none_kernel(tc, uT, wu, w_words, w_scales, gate, offs, out)
         on_vector, on_scalar = nc.vector.tensor_copy, nc.scalar.copy
 
         def round_u(h, split):
-            for copy, t0, t1 in ((on_vector, 0, split), (on_scalar, split, T)):
-                if t1 > t0:
-                    copy(
-                        pairs[h][:].rearrange("p (t e) -> p t e", e=2)[:, t0:t1, :],
-                        u_raw[h][:].rearrange("p e t -> p t e")[:, t0:t1, :],
-                    )
+            for i, (t0, t1) in enumerate(u_cuts[h]):
+                share = min(split, t1 - t0) if i == 0 else UB[h]
+                for copy, a, b in ((on_vector, 0, share), (on_scalar, share, t1 - t0)):
+                    if b > a:
+                        copy(
+                            pairs[h][:].rearrange("p (t e) -> p t e", e=2)[:, t0 + a : t0 + b, :],
+                            u_raw[h][i][:].rearrange("p e t -> p t e")[:, a:b, :],
+                        )
 
         def quantize(codes, scales, values):
             nc.vector.quantize_mx(out=codes.bitcast(FP8X4), scales=scales, in_=values)

@@ -20,7 +20,7 @@ G = K // 512
 IL = "step"
 GROUPS = (4, 2)
 G0ONE = False
-U0V = 512
+U0V = 448
 U1V = 0
 WV = (0, 0, 0, 40)
 QXM = "g"
@@ -38,6 +38,9 @@ WSPLIT = False
 OFFPOS = 1
 USPLIT = (False, True)
 UB = (256, 0)
+WCUT = 2
+WTAG = "wu_raw00"
+GTAG = "wu_raw064"
 
 
 def tile_moe_prv_lin_none_kernel(tc, uT, wu, w_words, w_scales, gate, offs, out):
@@ -54,11 +57,9 @@ def tile_moe_prv_lin_none_kernel(tc, uT, wu, w_words, w_scales, gate, offs, out)
         whole = (W0ONE, W1ONE)
         pieces = [[(0, 128)] if whole[g] else [(0, 64), (64, 128)] for g in range(G)]
         wu_raw = [
-            [keep.tile([P, 4, 4 * (m1 - m0)], F32, name="wu_raw%d%d" % (g, m0)) for m0, m1 in pieces[g]] for g in range(G)
+            [keep.tile([P, 4, 4 * (m1 - m0)], F32, name="wu_raw%d%d" % (g, m0), tag="wu_raw%d%d" % (g, m0), align_bytes=64) for m0, m1 in pieces[g]] for g in range(G)
         ]
-        words = keep.tile([P, E * G, 2 * N], U8, name="words", align_bytes=64)
         word_scales = keep.tile([P, E * G, N], U8, name="word_scales", align_bytes=64)
-        gates = keep.tile([P, T], F32, name="gates")
 
         nc.gpsimd.memset(word_scales[:].bitcast(I32), 0)
 
@@ -75,15 +76,9 @@ def tile_moe_prv_lin_none_kernel(tc, uT, wu, w_words, w_scales, gate, offs, out)
         for g in range(G):
             for i, (m0, m1) in enumerate(pieces[g]):
                 nc.sync.dma_start(wu_raw[g][i][:], wu_rows[:, :, 512 * g + 4 * m0 : 512 * g + 4 * m1])
-        scale_rows = w_scales.rearrange("e a q n -> q (e a) n").bitcast(I32)
-        for quad in range(4):
-            (nc.gpsimd if GSC else nc.sync).dma_start(
-                word_scales[32 * quad : 32 * quad + 4].bitcast(I32), scale_rows[4 * quad : 4 * quad + 4]
-            )
-        word_rows = w_words.rearrange("e a p n -> p (e a) n").bitcast(I32)
-        for e0, e1 in ((0, 3), (3, 6)) if WSPLIT else ((0, 6),):
-            nc.sync.dma_start(words[:, G * e0 : G * e1].bitcast(I32), word_rows[:, G * e0 : G * e1])
-            nc.sync.dma_start(gates[:, e0 * C : e1 * C], gate[:, e0 * C : e1 * C])
+        scale_rows = w_scales.rearrange("e a (quad r) n -> r quad (e a) n", r=4).bitcast(I32)
+        for r in range(4):
+            nc.sync.dma_start(word_scales[r:P:32].bitcast(I32), scale_rows[r])
 
         pad = 256 if G0ONE else 0
         pairs = [keep.tile([P, 2 * (T + (pad if h == 0 else 0))], BF16, name="pairs%d" % h) for h in range(2)]
@@ -231,10 +226,14 @@ def tile_moe_prv_lin_none_kernel(tc, uT, wu, w_words, w_scales, gate, offs, out)
         round_u(1, U1V)
         need(0)
         weights(0)
+        words = keep.tile([P, E * G, 2 * N], U8, name="words", tag=WTAG, align_bytes=64)
+        nc.scalar.dma_start(words[:].bitcast(I32), w_words.rearrange("e a p n -> p (e a) n").bitcast(I32))
         if not LATE:
             for e in range(E):
                 need(e)
         weights(1)
+        gates = keep.tile([P, T], F32, name="gates", tag=GTAG, align_bytes=64)
+        nc.scalar.dma_start(gates[:], gate)
         for e in range(LEAD):
             first_half(e)
         for e in range(E):

@@ -17,237 +17,210 @@ MULT = mybir.AluOpType.mult
 
 P = 128
 G = K // 512
-IL = "step"
-GROUPS = (4, 2)
-G0ONE = False
-U0V = 448
-U1V = 0
-WV = (0, 0, 0, 40)
-QXM = "g"
-SCM = (1, 1, 1, 1, 2)
-LEAD = 3
-SCL = 1
-VEV = ()
-W0ONE = False
-W1ONE = False
-LATE = True
-ALIAS = None
-R = (3, 2)
-GSC = True
-WSPLIT = False
-OFFPOS = 1
-USPLIT = (False, True)
-UB = (256, 0)
-WCUT = 2
-WTAG = "wu_raw00"
-GTAG = "wu_raw064"
+U_FIRST_ON_VECTOR = 512
+U_LAST_ON_VECTOR = 256
+FIRST_WORDS = 2
 
 
 def tile_moe_prv_lin_none_kernel(tc, uT, wu, w_words, w_scales, gate, offs, out):
     nc = tc.nc
-    first = [sum(GROUPS[:s]) for s in range(len(GROUPS))]
-    group_of = [s for s, n in enumerate(GROUPS) for i in range(n)]
+    on_vector, on_scalar = nc.vector.tensor_copy, nc.scalar.copy
     with ExitStack() as ctx:
         keep = ctx.enter_context(tc.tile_pool(name="keep", bufs=1))
         psum = ctx.enter_context(tc.psum_pool(name="psum", bufs=1))
 
+        def sbuf(name, shape, dtype, tag=None):
+            return keep.tile(shape, dtype, name=name, tag=tag or name, align_bytes=64)
+
         offsets = keep.tile([P, T // 16], U16, name="offsets")
-        u_cuts = [[(0, T // 2), (T // 2, T)] if USPLIT[h] else [(0, T)] for h in range(2)]
-        u_raw = [[keep.tile([P, 2, t1 - t0], F32, name="u_raw%d%d" % (h, t0)) for t0, t1 in u_cuts[h]] for h in range(2)]
-        whole = (W0ONE, W1ONE)
-        pieces = [[(0, 128)] if whole[g] else [(0, 64), (64, 128)] for g in range(G)]
-        wu_raw = [
-            [keep.tile([P, 4, 4 * (m1 - m0)], F32, name="wu_raw%d%d" % (g, m0), tag="wu_raw%d%d" % (g, m0), align_bytes=64) for m0, m1 in pieces[g]] for g in range(G)
-        ]
-        word_scales = keep.tile([P, E * G, N], U8, name="word_scales", align_bytes=64)
+        u_cuts = [[(0, T)], [(0, T // 2), (T // 2, T)]]
+        u_raw = [[sbuf("u_raw%d_%d" % (h, t0), [P, 2, t1 - t0], F32) for t0, t1 in u_cuts[h]] for h in range(2)]
+        wu_raw = [[sbuf("wu_raw%d_%d" % (g, i), [P, 4, 256], F32) for i in range(2)] for g in range(G)]
+        word_scales = sbuf("word_scales", [P, E * G, N], U8)
+        gates = sbuf("gates", [P, T], F32)
 
         nc.gpsimd.memset(word_scales[:].bitcast(I32), 0)
 
         u_rows = uT.rearrange("(p j) t -> p j t", j=4)
         wu_rows = wu.rearrange("(p j) k -> p j k", j=4)
-        if OFFPOS == 0:
-            nc.sync.dma_start(offsets[:], offs)
-        for i, (t0, t1) in enumerate(u_cuts[0]):
-            nc.sync.dma_start(u_raw[0][i][:], u_rows[:, 0:2, t0:t1])
-        if OFFPOS == 1:
-            nc.sync.dma_start(offsets[:], offs)
+        nc.sync.dma_start(u_raw[0][0][:], u_rows[:, 0:2, :])
+        nc.sync.dma_start(offsets[:], offs)
         for i, (t0, t1) in enumerate(u_cuts[1]):
             nc.sync.dma_start(u_raw[1][i][:], u_rows[:, 2:4, t0:t1])
         for g in range(G):
-            for i, (m0, m1) in enumerate(pieces[g]):
-                nc.sync.dma_start(wu_raw[g][i][:], wu_rows[:, :, 512 * g + 4 * m0 : 512 * g + 4 * m1])
+            for i in range(2):
+                nc.sync.dma_start(wu_raw[g][i][:], wu_rows[:, :, 512 * g + 256 * i : 512 * g + 256 * (i + 1)])
+        word_rows = w_words.rearrange("e a p n -> p (e a) n").bitcast(I32)
+        first_words = sbuf("first_words", [P, FIRST_WORDS * G, 2 * N], U8)
+        later_words = sbuf("later_words", [P, (E - FIRST_WORDS) * G, 2 * N], U8)
+        nc.sync.dma_start(first_words[:].bitcast(I32), word_rows[:, : FIRST_WORDS * G, :])
         scale_rows = w_scales.rearrange("e a (quad r) n -> r quad (e a) n", r=4).bitcast(I32)
         for r in range(4):
             nc.sync.dma_start(word_scales[r:P:32].bitcast(I32), scale_rows[r])
+        nc.sync.dma_start(gates[:], gate)
+        nc.sync.dma_start(later_words[:].bitcast(I32), word_rows[:, FIRST_WORDS * G :, :])
 
-        pad = 256 if G0ONE else 0
-        pairs = [keep.tile([P, 2 * (T + (pad if h == 0 else 0))], BF16, name="pairs%d" % h) for h in range(2)]
-        u_codes = keep.tile([P, T], U32, name="u_codes", align_bytes=64)
-        u_scales = keep.tile([P, T], U8, name="u_scales", align_bytes=64)
-        wu_bf = [keep.tile([P, 2048], BF16, name="wu_bf%d" % g, tag="wu_bf%d" % g, align_bytes=64) for g in range(G)]
-        wu_codes = [keep.tile([P, 512], U32, name="wu_codes%d" % g, align_bytes=64) for g in range(G)]
-        wu_scales = [keep.tile([P, 512], U8, name="wu_scales%d" % g, align_bytes=64) for g in range(G)]
-        x_bf = [keep.tile([P, G * 4 * C], BF16, name="x_bf%d" % e, align_bytes=64) for e in range(E)]
-        x_codes = [keep.tile([P, G * C], U32, name="x_codes%d" % e, align_bytes=64) for e in range(E)]
-        x_scales = [keep.tile([P, G * C], U8, name="x_scales%d" % e, align_bytes=64) for e in range(E)]
-        by_slot = keep.tile([P, T], F32, name="by_slot")
-        by_token = keep.tile([P, T], F32, name="by_token")
-        all_planes = keep.tile([P, 2, 2 * T], BF16, name="all_planes")
-        all_slots = keep.tile([P, 4 * T], BF16, name="all_slots", align_bytes=64)
-        on_vector, on_scalar = nc.vector.tensor_copy, nc.scalar.copy
+        pairs = [sbuf("pairs%d" % h, [P, 2 * T], BF16) for h in range(2)]
+        slots, u_codes, u_scales = {}, {}, {}
+        wu_bf_first = sbuf("wu_bf_first", [P, 4, P, 4], BF16)
 
-        def round_u(h, split):
-            for i, (t0, t1) in enumerate(u_cuts[h]):
-                share = min(split, t1 - t0) if i == 0 else UB[h]
-                for copy, a, b in ((on_vector, 0, share), (on_scalar, share, t1 - t0)):
-                    if b > a:
-                        copy(
-                            pairs[h][:].rearrange("p (t e) -> p t e", e=2)[:, t0 + a : t0 + b, :],
-                            u_raw[h][i][:].rearrange("p e t -> p t e")[:, a:b, :],
-                        )
+        wu_codes = [sbuf("wu_codes%d" % g, [P, 512], U32) for g in range(G)]
+        wu_scales = [sbuf("wu_scales%d" % g, [P, 512], U8) for g in range(G)]
+        by_slot = sbuf("by_slot", [P, T], F32)
+        by_token = sbuf("by_token", [P, T], F32)
+
+        def round_u(copy, h, i, a, b):
+            t0 = u_cuts[h][i][0]
+            copy(
+                pairs[h][:].rearrange("p (t e) -> p t e", e=2)[:, t0 + a : t0 + b, :],
+                u_raw[h][i][:].rearrange("p e t -> p t e")[:, a:b, :],
+            )
+
+        def round_wu(copy, target, g, i, t0, t1):
+            copy(
+                target[:, :, 64 * i : 64 * (i + 1), :].rearrange("p t m j -> p m t j"),
+                wu_raw[g][i][:].rearrange("p j (m t) -> p t m j", t=4)[:, t0:t1].rearrange("p t m j -> p m t j"),
+            )
 
         def quantize(codes, scales, values):
             nc.vector.quantize_mx(out=codes.bitcast(FP8X4), scales=scales, in_=values)
 
-        def gather(h, c0, c1, planes, slot_major):
-            if IL == "step":
-                target = slot_major.bitcast(U32).rearrange("p (c h) -> p c h", h=2)[:, :, h]
-            else:
-                target = planes[:, h, :].bitcast(U32)
-            nc.vector.tensor_copy(target, pairs[h][:].bitcast(U32).indirect(offsets[:, c0 // 16 : c1 // 16]))
+        def slot_tile(group, values=None):
+            e0, e1 = group
+            slots[group] = sbuf("slots%d" % e0, [P, 4 * C * (e1 - e0)], BF16)[:] if values is None else values
 
-        def slots(s):
-            c0, c1 = first[s] * C, (first[s] + GROUPS[s]) * C
-            planes = all_planes[:, :, 2 * c0 : 2 * c1]
-            slot_major = all_slots[:, 4 * c0 : 4 * c1]
-            if ALIAS == ("gg", s) and IL != "step":
-                own_planes = keep.tile([P, 2, 2 * (c1 - c0)], BF16, name="own_planes", tag="wu_bf1", align_bytes=64)
-                planes = own_planes[:]
-            elif ALIAS == ("il", s) or ALIAS == ("gg", s):
-                own_slots = keep.tile([P, 4 * (c1 - c0)], BF16, name="own_slots", tag="wu_bf1", align_bytes=64)
-                slot_major = own_slots[:]
-            if not G0ONE:
-                gather(0, c0, c1, planes, slot_major)
-            elif s == 0:
-                gather(0, 0, T, all_planes[:], all_slots[:])
-            gather(1, c0, c1, planes, slot_major)
-            if IL != "step":
-                (on_vector if IL == "V" else on_scalar)(
-                    slot_major.rearrange("p (c h e) -> p c h e", h=2, e=2),
-                    planes.rearrange("p h (c e) -> p c h e", e=2),
-                )
-            quantize(u_codes[:, c0:c1], u_scales[:, c0:c1], slot_major)
+        def quantize_wu(g, values, t0, t1):
+            quantize(wu_codes[g][:, t0 * P : t1 * P], wu_scales[g][:, t0 * P : t1 * P], values.rearrange("p t m j -> p (t m j)"))
 
-        def weights(g):
-            for i, (m0, m1) in enumerate(pieces[g]):
-                split = WV[2 * g] + WV[2 * g + 1] if whole[g] else WV[2 * g + i]
-                for copy, a, b in ((on_vector, 0, split), (on_scalar, split, m1 - m0)):
-                    if b > a:
-                        copy(
-                            wu_bf[g][:].rearrange("p (t m j) -> p m t j", t=4, j=4)[:, m0 + a : m0 + b],
-                            wu_raw[g][i][:].rearrange("p j (m t) -> p m t j", t=4)[:, a:b],
-                        )
-            quantize(wu_codes[g][:], wu_scales[g][:], wu_bf[g][:])
+        def gather(h, group):
+            e0, e1 = group
+            target = slots[group].bitcast(U32).rearrange("p (c h) -> p c h", h=2)[:, :, h]
+            nc.vector.tensor_copy(target, pairs[h][:].bitcast(U32).indirect(offsets[:, e0 * C // 16 : e1 * C // 16]))
 
-        ring, y_ring = R
-        uses = []
-        y_uses = []
+        def quantize_u(group, tag=None):
+            e0, e1 = group
+            codes = sbuf("u_codes%d" % e0, [P, C * (e1 - e0)], U32, tag)
+            scales = sbuf("u_scales%d" % e0, [P, C * (e1 - e0)], U8)
+            for e in range(e0, e1):
+                u_codes[e] = codes[:, (e - e0) * C : (e - e0 + 1) * C]
+                u_scales[e] = scales[:, (e - e0) * C : (e - e0 + 1) * C]
+            quantize(codes[:], scales[:], slots[group])
 
-        def next_bank(shape, is_y):
-            if is_y and y_ring:
-                y_uses.append(0)
-                tag = "ybank%d" % ((len(y_uses) - 1) % y_ring)
-            else:
-                uses.append(0)
-                tag = "bank%d" % ((len(uses) - 1) % ring)
-            return psum.tile(shape, F32, name="bank", tag=tag)
+        x_bf, x_codes, x_scales = {}, {}, {}
 
-        def project(e, g):
-            bank = next_bank([P, 4, C], False)
+        def x_tiles(name, halves, tag=None, values=None):
+            if values is None:
+                values = sbuf("x_bf" + name, [P, len(halves) * 4 * C], BF16, tag)[:]
+            codes = sbuf("x_codes" + name, [P, len(halves) * C], U32)
+            scales = sbuf("x_scales" + name, [P, len(halves) * C], U8)
+            for n, half in enumerate(halves):
+                x_bf[half] = (values, n)
+                x_codes[half] = codes
+                x_scales[half] = scales
+
+        def project(e, g, bank_number, copy):
+            bank = psum.tile([P, 4, C], F32, name="bank", tag="bank%d" % bank_number)
             for t in range(4):
                 nc.tensor.matmul_mx(
                     out=bank[:, t, :],
                     lhsT=wu_codes[g][:, t * P : (t + 1) * P].bitcast(FP8X4),
                     lhsT_scale=wu_scales[g][:, t * P : (t + 1) * P],
-                    rhs=u_codes[:, e * C : (e + 1) * C].bitcast(FP8X4),
-                    rhs_scale=u_scales[:, e * C : (e + 1) * C],
+                    rhs=u_codes[e].bitcast(FP8X4),
+                    rhs_scale=u_scales[e],
                     start=True,
                     stop=True,
                 )
-            (on_vector if (e, g) in VEV else on_scalar)(
-                x_bf[e][:, g * 4 * C : (g + 1) * 4 * C].rearrange("p (c t) -> p c t", t=4),
+            values, n = x_bf[e, g]
+            copy(
+                values[:, n * 4 * C : (n + 1) * 4 * C].rearrange("p (c t) -> p c t", t=4),
                 bank[:].rearrange("p t c -> p c t"),
             )
 
-        def quantize_x(e, g0, g1):
-            quantize(x_codes[e][:, g0 * C : g1 * C], x_scales[e][:, g0 * C : g1 * C], x_bf[e][:, g0 * 4 * C : g1 * 4 * C])
+        def quantize_x(half, count=1):
+            values, n = x_bf[half]
+            quantize(
+                x_codes[half][:, n * C : (n + count) * C],
+                x_scales[half][:, n * C : (n + count) * C],
+                values[:, n * 4 * C : (n + count) * 4 * C],
+            )
 
-        def expert(e):
-            bank = next_bank([P, C], True)
+        def expert(e, bank_number):
+            bank = psum.tile([P, C], F32, name="bank", tag="bank%d" % bank_number)
+            words, first = (first_words, 0) if e < FIRST_WORDS else (later_words, FIRST_WORDS)
             for g in range(G):
+                n = x_bf[e, g][1]
                 nc.tensor.matmul_mx(
                     out=bank[:],
-                    lhsT=words[:, e * G + g, :].bitcast(FP4X4),
+                    lhsT=words[:, (e - first) * G + g, :].bitcast(FP4X4),
                     lhsT_scale=word_scales[:, e * G + g, :],
-                    rhs=x_codes[e][:, g * C : (g + 1) * C].bitcast(FP8X4),
-                    rhs_scale=x_scales[e][:, g * C : (g + 1) * C],
+                    rhs=x_codes[e, g][:, n * C : (n + 1) * C].bitcast(FP8X4),
+                    rhs_scale=x_scales[e, g][:, n * C : (n + 1) * C],
                     start=(g == 0),
                     stop=(g == G - 1),
                 )
             nc.scalar.copy(by_slot[:, e * C : (e + 1) * C], bank[:])
 
-        ends = {sum(SCM[: i + 1]) - 1: sum(SCM[:i]) for i in range(len(SCM))}
+        def scatter(e0, e1):
+            nc.vector.tensor_tensor(
+                by_token[:].indirect(offsets[:, e0 * C // 16 : e1 * C // 16]),
+                by_slot[:, e0 * C : e1 * C],
+                gates[:, e0 * C : e1 * C],
+                MULT,
+            )
 
-        def scatter(e):
-            if e in ends:
-                e0, e1 = ends[e], e + 1
-                nc.vector.tensor_tensor(
-                    by_token[:].indirect(offsets[:, e0 * C // 16 : e1 * C // 16]),
-                    by_slot[:, e0 * C : e1 * C],
-                    gates[:, e0 * C : e1 * C],
-                    MULT,
-                )
-
-        gathered = set()
-        projected = set()
-
-        def need(e):
-            if group_of[e] not in gathered:
-                gathered.add(group_of[e])
-                slots(group_of[e])
-
-        def first_half(e):
-            if e < E and e not in projected:
-                projected.add(e)
-                need(e)
-                project(e, 0)
-
-        round_u(0, U0V)
-        round_u(1, U1V)
-        need(0)
-        weights(0)
-        words = keep.tile([P, E * G, 2 * N], U8, name="words", tag=WTAG, align_bytes=64)
-        nc.scalar.dma_start(words[:].bitcast(I32), w_words.rearrange("e a p n -> p (e a) n").bitcast(I32))
-        if not LATE:
-            for e in range(E):
-                need(e)
-        weights(1)
-        gates = keep.tile([P, T], F32, name="gates", tag=GTAG, align_bytes=64)
-        nc.scalar.dma_start(gates[:], gate)
-        for e in range(LEAD):
-            first_half(e)
-        for e in range(E):
-            first_half(e)
-            project(e, 1)
-            if QXM == "e" or (QXM == "m" and 0 < e < E - 1):
-                quantize_x(e, 0, 2)
-            else:
-                quantize_x(e, 0, 1)
-                quantize_x(e, 1, 2)
-            expert(e)
-            first_half(e + LEAD)
-            if e >= SCL:
-                scatter(e - SCL)
-        for e in range(E - SCL, E):
-            scatter(e)
+        round_u(on_vector, 0, 0, 0, U_FIRST_ON_VECTOR)
+        round_u(on_scalar, 0, 0, U_FIRST_ON_VECTOR, T)
+        round_u(on_scalar, 1, 0, 0, T // 2)
+        round_u(on_vector, 1, 1, 0, U_LAST_ON_VECTOR)
+        round_u(on_scalar, 1, 1, U_LAST_ON_VECTOR, T // 2)
+        groups = ((0, 4), (4, 5))
+        for group in groups:
+            slot_tile(group)
+        for h in range(2):
+            for group in groups:
+                gather(h, group)
+        for group in groups:
+            quantize_u(group)
+        for i in range(2):
+            round_wu(on_scalar, wu_bf_first[:], 0, i, 0, 4)
+        quantize_wu(0, wu_bf_first[:], 0, 4)
+        wu_bf_second = sbuf("wu_bf_second", [P, 4, P, 4], BF16)
+        round_wu(on_scalar, wu_bf_second[:], 1, 0, 0, 4)
+        round_wu(on_vector, wu_bf_second[:, 0:2], 1, 1, 0, 2)
+        round_wu(on_scalar, wu_bf_second[:, 2:4], 1, 1, 2, 4)
+        quantize_wu(1, wu_bf_second[:, 0:2], 0, 2)
+        quantize_wu(1, wu_bf_second[:, 2:4], 2, 4)
+        spent = sbuf("spent", [P, 4 * 4 * C], BF16, tag="wu_raw1_1")
+        slot_tile((5, 6), spent[:, : 4 * C])
+        x_tiles("_early", [(e, 0) for e in range(3)], values=spent[:, 4 * C :])
+        x_tiles("_01", [(0, 1)])
+        x_tiles("_11", [(1, 1)])
+        project(0, 0, 0, on_scalar)
+        project(1, 0, 1, on_scalar)
+        for h in range(2):
+            gather(h, (5, 6))
+        quantize_x((0, 0), 2)
+        project(0, 1, 2, on_scalar)
+        quantize_x((0, 1))
+        quantize_u((5, 6), tag="x_bf_01")
+        project(1, 1, 3, on_scalar)
+        quantize_x((1, 1))
+        project(2, 0, 1, on_scalar)
+        quantize_x((2, 0))
+        expert(0, 6)
+        scatter(0, 1)
+        x_tiles("_21", [(2, 1)], tag="x_codes_01")
+        project(2, 1, 5, on_scalar)
+        quantize_x((2, 1))
+        expert(1, 7)
+        scatter(1, 2)
+        for e in range(3, E):
+            x_tiles("_%d" % e, [(e, 0), (e, 1)])
+            for g in range(G):
+                project(e, g, (6, 5, 7)[(2 * e + g) % 3], on_scalar)
+            quantize_x((e, 0), 2)
+            expert(e - 1, (0, 2, 3)[e - 3])
+            scatter(e - 1, e)
+        expert(5, 4)
+        scatter(5, 6)
         nc.sync.dma_start(out, by_token[:])

@@ -17,8 +17,9 @@ MULT = mybir.AluOpType.mult
 
 P = 128
 G = K // 512
+PIECE = 256
 U_FIRST_ON_VECTOR = 512
-U_LAST_ON_VECTOR = 256
+M_LAST_ON_SCALAR = 24
 FIRST_WORDS = 2
 
 
@@ -27,15 +28,20 @@ def tile_moe_prv_lin_none_kernel(tc, uT, wu, w_words, w_scales, gate, offs, out)
     on_vector, on_scalar = nc.vector.tensor_copy, nc.scalar.copy
     with ExitStack() as ctx:
         keep = ctx.enter_context(tc.tile_pool(name="keep", bufs=1))
+        shared = ctx.enter_context(tc.tile_pool(name="shared", bufs=1))
         psum = ctx.enter_context(tc.psum_pool(name="psum", bufs=1))
 
         def sbuf(name, shape, dtype, tag=None):
             return keep.tile(shape, dtype, name=name, tag=tag or name, align_bytes=64)
 
+        def overlaid(name, shape, dtype, start):
+            return shared.tile(shape, dtype, name=name, align_bytes=64, offset=start)
+
         offsets = keep.tile([P, T // 16], U16, name="offsets")
         u_cuts = [[(0, T)], [(0, T // 2), (T // 2, T)]]
         u_raw = [[sbuf("u_raw%d_%d" % (h, t0), [P, 2, t1 - t0], F32) for t0, t1 in u_cuts[h]] for h in range(2)]
-        wu_raw = [[sbuf("wu_raw%d_%d" % (g, i), [P, 4, 256], F32) for i in range(2)] for g in range(G)]
+        wu_raw = [sbuf("wu_raw%d" % i, [P, 4, PIECE], F32) for i in range(3)]
+        wu_raw.append(overlaid("wu_raw3", [P, 4, PIECE], F32, 0))
         word_scales = sbuf("word_scales", [P, E * G, N], U8)
         gates = sbuf("gates", [P, T], F32)
 
@@ -43,13 +49,13 @@ def tile_moe_prv_lin_none_kernel(tc, uT, wu, w_words, w_scales, gate, offs, out)
 
         u_rows = uT.rearrange("(p j) t -> p j t", j=4)
         wu_rows = wu.rearrange("(p j) k -> p j k", j=4)
-        nc.sync.dma_start(u_raw[0][0][:], u_rows[:, 0:2, :])
-        nc.sync.dma_start(offsets[:], offs)
-        for i, (t0, t1) in enumerate(u_cuts[1]):
-            nc.sync.dma_start(u_raw[1][i][:], u_rows[:, 2:4, t0:t1])
-        for g in range(G):
-            for i in range(2):
-                nc.sync.dma_start(wu_raw[g][i][:], wu_rows[:, :, 512 * g + 256 * i : 512 * g + 256 * (i + 1)])
+        for h in range(2):
+            for i, (t0, t1) in enumerate(u_cuts[h]):
+                nc.sync.dma_start(u_raw[h][i][:], u_rows[:, 2 * h : 2 * h + 2, t0:t1])
+            if h == 0:
+                nc.sync.dma_start(offsets[:], offs)
+        for i in range(K // PIECE):
+            nc.sync.dma_start(wu_raw[i][:], wu_rows[:, :, PIECE * i : PIECE * (i + 1)])
         word_rows = w_words.rearrange("e a p n -> p (e a) n").bitcast(I32)
         first_words = sbuf("first_words", [P, FIRST_WORDS * G, 2 * N], U8)
         later_words = sbuf("later_words", [P, (E - FIRST_WORDS) * G, 2 * N], U8)
@@ -61,13 +67,13 @@ def tile_moe_prv_lin_none_kernel(tc, uT, wu, w_words, w_scales, gate, offs, out)
         nc.sync.dma_start(later_words[:].bitcast(I32), word_rows[:, FIRST_WORDS * G :, :])
 
         pairs = [sbuf("pairs%d" % h, [P, 2 * T], BF16) for h in range(2)]
-        slots, u_codes, u_scales = {}, {}, {}
-        wu_bf_first = sbuf("wu_bf_first", [P, 4, P, 4], BF16)
-
-        wu_codes = [sbuf("wu_codes%d" % g, [P, 512], U32) for g in range(G)]
-        wu_scales = [sbuf("wu_scales%d" % g, [P, 512], U8) for g in range(G)]
         by_slot = sbuf("by_slot", [P, T], F32)
         by_token = sbuf("by_token", [P, T], F32)
+        u_codes, u_scales = {}, {}
+        x_bf, x_codes, x_scales = {}, {}, {}
+
+        def slot_offsets(e0, e1):
+            return offsets[:, e0 * C // 16 : e1 * C // 16]
 
         def round_u(copy, h, i, a, b):
             t0 = u_cuts[h][i][0]
@@ -76,49 +82,34 @@ def tile_moe_prv_lin_none_kernel(tc, uT, wu, w_words, w_scales, gate, offs, out)
                 u_raw[h][i][:].rearrange("p e t -> p t e")[:, a:b, :],
             )
 
-        def round_wu(copy, target, g, i, t0, t1):
+        def round_wu(copy, rounded, i, t0, t1, a=0, b=64):
+            m0 = 64 * (i % 2)
             copy(
-                target[:, :, 64 * i : 64 * (i + 1), :].rearrange("p t m j -> p m t j"),
-                wu_raw[g][i][:].rearrange("p j (m t) -> p t m j", t=4)[:, t0:t1].rearrange("p t m j -> p m t j"),
+                rounded[:, t0:t1, m0 + a : m0 + b, :].rearrange("p t m j -> p m t j"),
+                wu_raw[i][:].rearrange("p j (m t) -> p t m j", t=4)[:, t0:t1, a:b].rearrange("p t m j -> p m t j"),
             )
 
         def quantize(codes, scales, values):
             nc.vector.quantize_mx(out=codes.bitcast(FP8X4), scales=scales, in_=values)
 
-        def slot_tile(group, values=None):
-            e0, e1 = group
-            slots[group] = sbuf("slots%d" % e0, [P, 4 * C * (e1 - e0)], BF16)[:] if values is None else values
+        def gather(target, h, e0, e1):
+            on_vector(target, pairs[h][:].bitcast(U32).indirect(slot_offsets(e0, e1)))
 
-        def quantize_wu(g, values, t0, t1):
-            quantize(wu_codes[g][:, t0 * P : t1 * P], wu_scales[g][:, t0 * P : t1 * P], values.rearrange("p t m j -> p (t m j)"))
+        def gather_woven(slots, h, e0, e1):
+            gather(slots.bitcast(U32).rearrange("p (c h) -> p c h", h=2)[:, :, h], h, e0, e1)
 
-        def gather(h, group):
-            e0, e1 = group
-            target = slots[group].bitcast(U32).rearrange("p (c h) -> p c h", h=2)[:, :, h]
-            nc.vector.tensor_copy(target, pairs[h][:].bitcast(U32).indirect(offsets[:, e0 * C // 16 : e1 * C // 16]))
-
-        def quantize_u(group, tag=None):
-            e0, e1 = group
-            codes = sbuf("u_codes%d" % e0, [P, C * (e1 - e0)], U32, tag)
+        def quantize_u(slots, e0, e1, codes):
             scales = sbuf("u_scales%d" % e0, [P, C * (e1 - e0)], U8)
             for e in range(e0, e1):
                 u_codes[e] = codes[:, (e - e0) * C : (e - e0 + 1) * C]
                 u_scales[e] = scales[:, (e - e0) * C : (e - e0 + 1) * C]
-            quantize(codes[:], scales[:], slots[group])
+            quantize(codes[:], scales[:], slots)
 
-        x_bf, x_codes, x_scales = {}, {}, {}
+        def quantize_wu(g, rounded, t0, t1):
+            columns = slice(t0 * P, t1 * P)
+            quantize(wu_codes[g][:, columns], wu_scales[g][:, columns], rounded[:, t0:t1].rearrange("p t m j -> p (t m j)"))
 
-        def x_tiles(name, halves, tag=None, values=None):
-            if values is None:
-                values = sbuf("x_bf" + name, [P, len(halves) * 4 * C], BF16, tag)[:]
-            codes = sbuf("x_codes" + name, [P, len(halves) * C], U32)
-            scales = sbuf("x_scales" + name, [P, len(halves) * C], U8)
-            for n, half in enumerate(halves):
-                x_bf[half] = (values, n)
-                x_codes[half] = codes
-                x_scales[half] = scales
-
-        def project(e, g, bank_number, copy):
+        def project(e, g, bank_number):
             bank = psum.tile([P, 4, C], F32, name="bank", tag="bank%d" % bank_number)
             for t in range(4):
                 nc.tensor.matmul_mx(
@@ -130,97 +121,86 @@ def tile_moe_prv_lin_none_kernel(tc, uT, wu, w_words, w_scales, gate, offs, out)
                     start=True,
                     stop=True,
                 )
-            values, n = x_bf[e, g]
-            copy(
-                values[:, n * 4 * C : (n + 1) * 4 * C].rearrange("p (c t) -> p c t", t=4),
-                bank[:].rearrange("p t c -> p c t"),
-            )
+            on_scalar(x_bf[e, g].rearrange("p (c t) -> p c t", t=4), bank[:].rearrange("p t c -> p c t"))
 
-        def quantize_x(half, count=1):
-            values, n = x_bf[half]
-            quantize(
-                x_codes[half][:, n * C : (n + count) * C],
-                x_scales[half][:, n * C : (n + count) * C],
-                values[:, n * 4 * C : (n + count) * 4 * C],
-            )
+        def make_x(name, halves, banks, values):
+            codes = sbuf("x_codes" + name, [P, len(halves) * C], U32)
+            scales = sbuf("x_scales" + name, [P, len(halves) * C], U8)
+            for n, (half, bank_number) in enumerate(zip(halves, banks)):
+                x_bf[half] = values[:, n * 4 * C : (n + 1) * 4 * C]
+                x_codes[half] = codes[:, n * C : (n + 1) * C]
+                x_scales[half] = scales[:, n * C : (n + 1) * C]
+                project(*half, bank_number)
+            quantize(codes[:], scales[:], values[:])
+
+        def make_half(e, g, bank_number, tag=None):
+            name = "_%d%d" % (e, g)
+            make_x(name, [(e, g)], [bank_number], sbuf("x_bf" + name, [P, 4 * C], BF16, tag))
 
         def expert(e, bank_number):
             bank = psum.tile([P, C], F32, name="bank", tag="bank%d" % bank_number)
             words, first = (first_words, 0) if e < FIRST_WORDS else (later_words, FIRST_WORDS)
             for g in range(G):
-                n = x_bf[e, g][1]
                 nc.tensor.matmul_mx(
                     out=bank[:],
                     lhsT=words[:, (e - first) * G + g, :].bitcast(FP4X4),
                     lhsT_scale=word_scales[:, e * G + g, :],
-                    rhs=x_codes[e, g][:, n * C : (n + 1) * C].bitcast(FP8X4),
-                    rhs_scale=x_scales[e, g][:, n * C : (n + 1) * C],
+                    rhs=x_codes[e, g].bitcast(FP8X4),
+                    rhs_scale=x_scales[e, g],
                     start=(g == 0),
                     stop=(g == G - 1),
                 )
-            nc.scalar.copy(by_slot[:, e * C : (e + 1) * C], bank[:])
-
-        def scatter(e0, e1):
-            nc.vector.tensor_tensor(
-                by_token[:].indirect(offsets[:, e0 * C // 16 : e1 * C // 16]),
-                by_slot[:, e0 * C : e1 * C],
-                gates[:, e0 * C : e1 * C],
-                MULT,
-            )
+            slots = slice(e * C, (e + 1) * C)
+            on_scalar(by_slot[:, slots], bank[:])
+            nc.vector.tensor_tensor(by_token[:].indirect(slot_offsets(e, e + 1)), by_slot[:, slots], gates[:, slots], MULT)
 
         round_u(on_vector, 0, 0, 0, U_FIRST_ON_VECTOR)
         round_u(on_scalar, 0, 0, U_FIRST_ON_VECTOR, T)
-        round_u(on_scalar, 1, 0, 0, T // 2)
-        round_u(on_vector, 1, 1, 0, U_LAST_ON_VECTOR)
-        round_u(on_scalar, 1, 1, U_LAST_ON_VECTOR, T // 2)
-        groups = ((0, 4), (4, 5))
-        for group in groups:
-            slot_tile(group)
-        for h in range(2):
-            for group in groups:
-                gather(h, group)
-        for group in groups:
-            quantize_u(group)
         for i in range(2):
-            round_wu(on_scalar, wu_bf_first[:], 0, i, 0, 4)
-        quantize_wu(0, wu_bf_first[:], 0, 4)
-        wu_bf_second = sbuf("wu_bf_second", [P, 4, P, 4], BF16)
-        round_wu(on_scalar, wu_bf_second[:], 1, 0, 0, 4)
-        round_wu(on_vector, wu_bf_second[:, 0:2], 1, 1, 0, 2)
-        round_wu(on_scalar, wu_bf_second[:, 2:4], 1, 1, 2, 4)
-        quantize_wu(1, wu_bf_second[:, 0:2], 0, 2)
-        quantize_wu(1, wu_bf_second[:, 2:4], 2, 4)
-        spent = sbuf("spent", [P, 4 * 4 * C], BF16, tag="wu_raw1_1")
-        slot_tile((5, 6), spent[:, : 4 * C])
-        x_tiles("_early", [(e, 0) for e in range(3)], values=spent[:, 4 * C :])
-        x_tiles("_01", [(0, 1)])
-        x_tiles("_11", [(1, 1)])
-        project(0, 0, 0, on_scalar)
-        project(1, 0, 1, on_scalar)
-        for h in range(2):
-            gather(h, (5, 6))
-        quantize_x((0, 0), 2)
-        project(0, 1, 2, on_scalar)
-        quantize_x((0, 1))
-        quantize_u((5, 6), tag="x_bf_01")
-        project(1, 1, 3, on_scalar)
-        quantize_x((1, 1))
-        project(2, 0, 1, on_scalar)
-        quantize_x((2, 0))
+            round_u(on_scalar, 1, i, 0, T // 2)
+        first_slots = sbuf("first_slots", [P, 4 * 4 * C], BF16)
+        late = sbuf("late", [P, 10 * C], U32)
+        gather_woven(first_slots[:], 0, 0, 4)
+        gather(late[:, : 2 * C], 0, 4, 6)
+        gather_woven(first_slots[:, : 8 * C], 1, 0, 2)
+        gather_woven(first_slots[:, 8 * C :], 1, 2, 4)
+        quantize_u(first_slots[:, : 8 * C], 0, 2, sbuf("u_codes0", [P, 2 * C], U32))
+
+        wu_codes = [sbuf("wu_codes%d" % g, [P, 4 * P], U32) for g in range(G)]
+        wu_scales = [sbuf("wu_scales%d" % g, [P, 4 * P], U8) for g in range(G)]
+        first_half = sbuf("first_half", [P, 4, P, 4], BF16)
+        second_half = late[:, 2 * C :].bitcast(BF16).rearrange("p (t m j) -> p t m j", t=4, j=4)
+        round_wu(on_scalar, first_half[:], 0, 0, 4)
+        round_wu(on_vector, first_half[:], 1, 0, 2)
+        round_wu(on_scalar, first_half[:], 1, 2, 4)
+        for t0 in (0, 2):
+            quantize_wu(0, first_half[:], t0, t0 + 2)
+        round_wu(on_scalar, second_half, 2, 0, 4)
+        round_wu(on_vector, second_half, 3, 0, 2)
+        round_wu(on_scalar, second_half, 3, 2, 4, 0, M_LAST_ON_SCALAR)
+        round_wu(on_vector, second_half, 3, 2, 4, M_LAST_ON_SCALAR, 64)
+        for t0 in (0, 2):
+            quantize_wu(1, second_half, t0, t0 + 2)
+
+        quantize_u(first_slots[:, 8 * C :], 2, 4, overlaid("u_codes2", [P, 2 * C], U32, 2 * 8 * C))
+        make_x("_early", [(0, 0), (1, 0)], [0, 1], overlaid("x_bf_early", [P, 8 * C], BF16, 0))
+        gather(late[:, 2 * C : 4 * C], 1, 4, 6)
+        make_half(0, 1, 2)
+        make_half(1, 1, 3)
+        last_slots = sbuf("last_slots", [P, 8 * C], BF16, tag="x_bf_01")
+        on_vector(
+            last_slots[:].bitcast(I32).rearrange("p (c h) -> p c h", h=2),
+            late[:, : 4 * C].bitcast(I32).rearrange("p (h c) -> p c h", h=2),
+        )
+        quantize_u(last_slots[:], 4, 6, sbuf("u_codes4", [P, 2 * C], U32))
+        make_half(2, 0, 1)
         expert(0, 6)
-        scatter(0, 1)
-        x_tiles("_21", [(2, 1)], tag="x_codes_01")
-        project(2, 1, 5, on_scalar)
-        quantize_x((2, 1))
+        make_half(2, 1, 5, tag="x_codes_01")
         expert(1, 7)
-        scatter(1, 2)
+        projection_banks, result_banks = (6, 5, 7), (0, 2, 3, 4)
         for e in range(3, E):
-            x_tiles("_%d" % e, [(e, 0), (e, 1)])
-            for g in range(G):
-                project(e, g, (6, 5, 7)[(2 * e + g) % 3], on_scalar)
-            quantize_x((e, 0), 2)
-            expert(e - 1, (0, 2, 3)[e - 3])
-            scatter(e - 1, e)
-        expert(5, 4)
-        scatter(5, 6)
+            banks = [projection_banks[(G * e + g) % 3] for g in range(G)]
+            make_x("_%d" % e, [(e, g) for g in range(G)], banks, sbuf("x_bf_%d" % e, [P, G * 4 * C], BF16))
+            expert(e - 1, result_banks[e - 3])
+        expert(E - 1, result_banks[-1])
         nc.sync.dma_start(out, by_token[:])

@@ -14,13 +14,14 @@ U8 = mybir.dt.uint8
 FP8X4 = mybir.dt.float8_e4m3fn_x4
 FP4X4 = mybir.dt.float4_e2m1fn_x4
 MULT = mybir.AluOpType.mult
+ADD = mybir.AluOpType.add
+COPY = mybir.ActivationFunctionType.Copy
 
 P = 128
 G = K // 512
 PIECE = 256
 U_FIRST_ON_VECTOR = 512
-M_LAST_ON_SCALAR = 24
-FIRST_WORDS = 2
+STORES = 3
 
 
 def tile_moe_prv_lin_none_kernel(tc, uT, wu, w_words, w_scales, gate, offs, out):
@@ -38,14 +39,17 @@ def tile_moe_prv_lin_none_kernel(tc, uT, wu, w_words, w_scales, gate, offs, out)
             return shared.tile(shape, dtype, name=name, align_bytes=64, offset=start)
 
         offsets = keep.tile([P, T // 16], U16, name="offsets")
-        u_cuts = [[(0, T)], [(0, T // 2), (T // 2, T)]]
+        u_cuts = [[(0, T)], [(0, 256), (256, 512), (512, T)]]
         u_raw = [[sbuf("u_raw%d_%d" % (h, t0), [P, 2, t1 - t0], F32) for t0, t1 in u_cuts[h]] for h in range(2)]
-        wu_raw = [sbuf("wu_raw%d" % i, [P, 4, PIECE], F32) for i in range(3)]
-        wu_raw.append(overlaid("wu_raw3", [P, 4, PIECE], F32, 0))
+        raw_bytes = 4 * PIECE * 4
+        wu_raw = [overlaid("wu_raw%d" % i, [P, 4, PIECE], F32, i * raw_bytes) for i in range(4)]
         word_scales = sbuf("word_scales", [P, E * G, N], U8)
         gates = sbuf("gates", [P, T], F32)
+        windows = [sbuf("window%d" % i, [P, T], F32) for i in range(2)]
 
         nc.gpsimd.memset(word_scales[:].bitcast(I32), 0)
+        for window in windows:
+            nc.gpsimd.memset(window[:], 0.0)
 
         u_rows = uT.rearrange("(p j) t -> p j t", j=4)
         wu_rows = wu.rearrange("(p j) k -> p j k", j=4)
@@ -57,18 +61,15 @@ def tile_moe_prv_lin_none_kernel(tc, uT, wu, w_words, w_scales, gate, offs, out)
         for i in range(K // PIECE):
             nc.sync.dma_start(wu_raw[i][:], wu_rows[:, :, PIECE * i : PIECE * (i + 1)])
         word_rows = w_words.rearrange("e a p n -> p (e a) n").bitcast(I32)
-        first_words = sbuf("first_words", [P, FIRST_WORDS * G, 2 * N], U8)
-        later_words = sbuf("later_words", [P, (E - FIRST_WORDS) * G, 2 * N], U8)
-        nc.sync.dma_start(first_words[:].bitcast(I32), word_rows[:, : FIRST_WORDS * G, :])
+        words = sbuf("words", [P, E * G, 2 * N], U8)
+        nc.sync.dma_start(gates[:], gate)
+        nc.sync.dma_start(words[:].bitcast(I32), word_rows)
         scale_rows = w_scales.rearrange("e a (quad r) n -> r quad (e a) n", r=4).bitcast(I32)
         for r in range(4):
             nc.sync.dma_start(word_scales[r:P:32].bitcast(I32), scale_rows[r])
-        nc.sync.dma_start(gates[:], gate)
-        nc.sync.dma_start(later_words[:].bitcast(I32), word_rows[:, FIRST_WORDS * G :, :])
 
         pairs = [sbuf("pairs%d" % h, [P, 2 * T], BF16) for h in range(2)]
-        by_slot = sbuf("by_slot", [P, T], F32)
-        by_token = sbuf("by_token", [P, T], F32)
+        planes = sbuf("planes", [P, 2 * T], U32)
         u_codes, u_scales = {}, {}
         x_bf, x_codes, x_scales = {}, {}, {}
 
@@ -82,34 +83,40 @@ def tile_moe_prv_lin_none_kernel(tc, uT, wu, w_words, w_scales, gate, offs, out)
                 u_raw[h][i][:].rearrange("p e t -> p t e")[:, a:b, :],
             )
 
-        def round_wu(copy, rounded, i, t0, t1, a=0, b=64):
+        def round_wu(copy, i, t0, t1):
             m0 = 64 * (i % 2)
             copy(
-                rounded[:, t0:t1, m0 + a : m0 + b, :].rearrange("p t m j -> p m t j"),
-                wu_raw[i][:].rearrange("p j (m t) -> p t m j", t=4)[:, t0:t1, a:b].rearrange("p t m j -> p m t j"),
+                wu_bf[i // 2][:, t0:t1, m0 : m0 + 64, :].rearrange("p t m j -> p m t j"),
+                wu_raw[i][:].rearrange("p j (m t) -> p m t j", t=4)[:, :, t0:t1, :],
             )
 
         def quantize(codes, scales, values):
             nc.vector.quantize_mx(out=codes.bitcast(FP8X4), scales=scales, in_=values)
 
-        def gather(target, h, e0, e1):
-            on_vector(target, pairs[h][:].bitcast(U32).indirect(slot_offsets(e0, e1)))
+        def gather(h, e0, e1):
+            on_vector(planes[:, h * T + e0 * C : h * T + e1 * C], pairs[h][:].bitcast(U32).indirect(slot_offsets(e0, e1)))
 
-        def gather_woven(slots, h, e0, e1):
-            gather(slots.bitcast(U32).rearrange("p (c h) -> p c h", h=2)[:, :, h], h, e0, e1)
+        def weave(e0, start):
+            slots = overlaid("slots%d" % e0, [P, 8 * C], BF16, start)
+            on_scalar(
+                slots[:].bitcast(U32).rearrange("p (c h) -> p c h", h=2),
+                planes[:].rearrange("p (h c) -> p c h", h=2)[:, e0 * C : (e0 + 2) * C, :],
+            )
+            return slots
 
-        def quantize_u(slots, e0, e1, codes):
-            scales = sbuf("u_scales%d" % e0, [P, C * (e1 - e0)], U8)
-            for e in range(e0, e1):
+        def quantize_u(slots, e0):
+            codes = sbuf("u_codes%d" % e0, [P, 2 * C], U32)
+            scales = sbuf("u_scales%d" % e0, [P, 2 * C], U8)
+            for e in (e0, e0 + 1):
                 u_codes[e] = codes[:, (e - e0) * C : (e - e0 + 1) * C]
                 u_scales[e] = scales[:, (e - e0) * C : (e - e0 + 1) * C]
-            quantize(codes[:], scales[:], slots)
+            quantize(codes[:], scales[:], slots[:])
 
-        def quantize_wu(g, rounded, t0, t1):
+        def quantize_wu(g, t0, t1):
             columns = slice(t0 * P, t1 * P)
-            quantize(wu_codes[g][:, columns], wu_scales[g][:, columns], rounded[:, t0:t1].rearrange("p t m j -> p (t m j)"))
+            quantize(wu_codes[g][:, columns], wu_scales[g][:, columns], wu_bf[g][:, t0:t1].rearrange("p t m j -> p (t m j)"))
 
-        def project(e, g, bank_number):
+        def project(e, g, bank_number, copy, values):
             bank = psum.tile([P, 4, C], F32, name="bank", tag="bank%d" % bank_number)
             for t in range(4):
                 nc.tensor.matmul_mx(
@@ -121,86 +128,87 @@ def tile_moe_prv_lin_none_kernel(tc, uT, wu, w_words, w_scales, gate, offs, out)
                     start=True,
                     stop=True,
                 )
-            on_scalar(x_bf[e, g].rearrange("p (c t) -> p c t", t=4), bank[:].rearrange("p t c -> p c t"))
+            copy(values.rearrange("p (c t) -> p c t", t=4), bank[:].rearrange("p t c -> p c t"))
 
-        def make_x(name, halves, banks, values):
-            codes = sbuf("x_codes" + name, [P, len(halves) * C], U32)
+        def make_x(halves, values=None, codes_tag=None):
+            name = "_%d%d" % halves[0][:2]
+            if values is None:
+                values = sbuf("x_bf" + name, [P, len(halves) * 4 * C], BF16)
+            codes = sbuf("x_codes" + name, [P, len(halves) * C], U32, codes_tag)
             scales = sbuf("x_scales" + name, [P, len(halves) * C], U8)
-            for n, (half, bank_number) in enumerate(zip(halves, banks)):
-                x_bf[half] = values[:, n * 4 * C : (n + 1) * 4 * C]
-                x_codes[half] = codes[:, n * C : (n + 1) * C]
-                x_scales[half] = scales[:, n * C : (n + 1) * C]
-                project(*half, bank_number)
+            for n, (e, g, bank_number, copy) in enumerate(halves):
+                x_codes[e, g] = codes[:, n * C : (n + 1) * C]
+                x_scales[e, g] = scales[:, n * C : (n + 1) * C]
+                project(e, g, bank_number, copy, values[:, n * 4 * C : (n + 1) * 4 * C])
             quantize(codes[:], scales[:], values[:])
 
-        def make_half(e, g, bank_number, tag=None):
-            name = "_%d%d" % (e, g)
-            make_x(name, [(e, g)], [bank_number], sbuf("x_bf" + name, [P, 4 * C], BF16, tag))
+        def experts(e0, e1, bank_number):
+            bank = psum.tile([P, (e1 - e0) * C], F32, name="bank", tag="bank%d" % bank_number)
+            for e in range(e0, e1):
+                for g in range(G):
+                    nc.tensor.matmul_mx(
+                        out=bank[:, (e - e0) * C : (e - e0 + 1) * C],
+                        lhsT=words[:, e * G + g, :].bitcast(FP4X4),
+                        lhsT_scale=word_scales[:, e * G + g, :],
+                        rhs=x_codes[e, g].bitcast(FP8X4),
+                        rhs_scale=x_scales[e, g],
+                        start=(g == 0),
+                        stop=(g == G - 1),
+                    )
+            return bank
 
-        def expert(e, bank_number):
-            bank = psum.tile([P, C], F32, name="bank", tag="bank%d" % bank_number)
-            words, first = (first_words, 0) if e < FIRST_WORDS else (later_words, FIRST_WORDS)
-            for g in range(G):
-                nc.tensor.matmul_mx(
-                    out=bank[:],
-                    lhsT=words[:, (e - first) * G + g, :].bitcast(FP4X4),
-                    lhsT_scale=word_scales[:, e * G + g, :],
-                    rhs=x_codes[e, g].bitcast(FP8X4),
-                    rhs_scale=x_scales[e, g],
-                    start=(g == 0),
-                    stop=(g == G - 1),
-                )
-            slots = slice(e * C, (e + 1) * C)
-            on_scalar(by_slot[:, slots], bank[:])
-            nc.vector.tensor_tensor(by_token[:].indirect(slot_offsets(e, e + 1)), by_slot[:, slots], gates[:, slots], MULT)
+        def gated(e0, e1, bank_number):
+            bank = experts(e0, e1, bank_number)
+            result = sbuf("result%d" % e0, [P, (e1 - e0) * C], F32)
+            nc.vector.tensor_tensor(result[:], bank[:], gates[:, e0 * C : e1 * C], MULT)
+            return result
+
+        def scatter_on_vector(e, values):
+            on_vector(windows[0][:].indirect(slot_offsets(e, e + 1)), values)
+
+        wu_bf = [sbuf("wu_bf%d" % g, [P, 4, P, 4], BF16) for g in range(G)]
+        wu_codes = [sbuf("wu_codes%d" % g, [P, 4 * P], U32) for g in range(G)]
+        wu_scales = [sbuf("wu_scales%d" % g, [P, 4 * P], U8) for g in range(G)]
 
         round_u(on_vector, 0, 0, 0, U_FIRST_ON_VECTOR)
         round_u(on_scalar, 0, 0, U_FIRST_ON_VECTOR, T)
-        for i in range(2):
-            round_u(on_scalar, 1, i, 0, T // 2)
-        first_slots = sbuf("first_slots", [P, 4 * 4 * C], BF16)
-        late = sbuf("late", [P, 10 * C], U32)
-        gather_woven(first_slots[:], 0, 0, 4)
-        gather(late[:, : 2 * C], 0, 4, 6)
-        gather_woven(first_slots[:, : 8 * C], 1, 0, 2)
-        gather_woven(first_slots[:, 8 * C :], 1, 2, 4)
-        quantize_u(first_slots[:, : 8 * C], 0, 2, sbuf("u_codes0", [P, 2 * C], U32))
+        for i in range(3):
+            round_u(on_scalar, 1, i, 0, 256)
+        for h in range(2):
+            gather(h, 0, 4)
+            gather(h, 4, 6)
+        round_wu(on_scalar, 0, 0, 4)
+        slots0 = weave(0, 0)
+        slots2 = weave(2, raw_bytes // 2)
+        round_wu(on_vector, 1, 0, 2)
+        round_wu(on_vector, 1, 2, 4)
+        quantize_wu(0, 0, 2)
+        quantize_u(slots0, 0)
+        quantize_wu(0, 2, 4)
+        quantize_u(slots2, 2)
+        round_wu(on_scalar, 2, 0, 4)
+        slots4 = weave(4, 2 * raw_bytes)
+        round_wu(on_vector, 3, 0, 2)
+        round_wu(on_vector, 3, 2, 4)
+        quantize_wu(1, 0, 2)
+        quantize_wu(1, 2, 4)
+        quantize_u(slots4, 4)
 
-        wu_codes = [sbuf("wu_codes%d" % g, [P, 4 * P], U32) for g in range(G)]
-        wu_scales = [sbuf("wu_scales%d" % g, [P, 4 * P], U8) for g in range(G)]
-        first_half = sbuf("first_half", [P, 4, P, 4], BF16)
-        second_half = late[:, 2 * C :].bitcast(BF16).rearrange("p (t m j) -> p t m j", t=4, j=4)
-        round_wu(on_scalar, first_half[:], 0, 0, 4)
-        round_wu(on_vector, first_half[:], 1, 0, 2)
-        round_wu(on_scalar, first_half[:], 1, 2, 4)
-        for t0 in (0, 2):
-            quantize_wu(0, first_half[:], t0, t0 + 2)
-        round_wu(on_scalar, second_half, 2, 0, 4)
-        round_wu(on_vector, second_half, 3, 0, 2)
-        round_wu(on_scalar, second_half, 3, 2, 4, 0, M_LAST_ON_SCALAR)
-        round_wu(on_vector, second_half, 3, 2, 4, M_LAST_ON_SCALAR, 64)
-        for t0 in (0, 2):
-            quantize_wu(1, second_half, t0, t0 + 2)
-
-        quantize_u(first_slots[:, 8 * C :], 2, 4, overlaid("u_codes2", [P, 2 * C], U32, 2 * 8 * C))
-        make_x("_early", [(0, 0), (1, 0)], [0, 1], overlaid("x_bf_early", [P, 8 * C], BF16, 0))
-        gather(late[:, 2 * C : 4 * C], 1, 4, 6)
-        make_half(0, 1, 2)
-        make_half(1, 1, 3)
-        last_slots = sbuf("last_slots", [P, 8 * C], BF16, tag="x_bf_01")
-        on_vector(
-            last_slots[:].bitcast(I32).rearrange("p (c h) -> p c h", h=2),
-            late[:, : 4 * C].bitcast(I32).rearrange("p (h c) -> p c h", h=2),
-        )
-        quantize_u(last_slots[:], 4, 6, sbuf("u_codes4", [P, 2 * C], U32))
-        make_half(2, 0, 1)
-        expert(0, 6)
-        make_half(2, 1, 5, tag="x_codes_01")
-        expert(1, 7)
-        projection_banks, result_banks = (6, 5, 7), (0, 2, 3, 4)
-        for e in range(3, E):
-            banks = [projection_banks[(G * e + g) % 3] for g in range(G)]
-            make_x("_%d" % e, [(e, g) for g in range(G)], banks, sbuf("x_bf_%d" % e, [P, G * 4 * C], BF16))
-            expert(e - 1, result_banks[e - 3])
-        expert(E - 1, result_banks[-1])
-        nc.sync.dma_start(out, by_token[:])
+        make_x([(0, 0, 0, on_scalar), (1, 0, 1, on_scalar)])
+        make_x([(2, 0, 2, on_scalar), (3, 0, 3, on_vector)], overlaid("x_bf_20", [P, 8 * C], BF16, 3 * raw_bytes))
+        make_x([(0, 1, 4, on_vector), (1, 1, 5, on_scalar)])
+        make_x([(2, 1, 6, on_scalar), (3, 1, 7, on_scalar)])
+        first_results = gated(0, 4, 4)
+        make_x([(4, 0, 0, on_scalar), (4, 1, 1, on_scalar)], codes_tag="x_codes_21")
+        scatter_on_vector(3, first_results[:, 3 * C :])
+        fifth_result = gated(4, 5, 5)
+        make_x([(5, 0, 2, on_scalar), (5, 1, 3, on_scalar)], codes_tag="x_codes_21")
+        scatter_on_vector(4, fifth_result[:])
+        nc.scalar.activation(windows[1][:].indirect(slot_offsets(0, 3)), first_results[:, : 3 * C], COPY)
+        scatter_on_vector(5, gated(5, 6, 6)[:])
+        width = T // STORES
+        for i in range(STORES):
+            columns = slice(i * width, (i + 1) * width)
+            total = sbuf("total%d" % i, [P, width], F32)
+            nc.vector.tensor_tensor(total[:], windows[0][:, columns], windows[1][:, columns], ADD)
+            nc.sync.dma_start(out[:, columns], total[:])

@@ -21,6 +21,7 @@ P = 128
 G = K // 512
 PIECE = 256
 U_FIRST_ON_VECTOR = 512
+FIRST_ON_VECTOR = 96
 STORES = 3
 
 
@@ -159,13 +160,15 @@ def tile_moe_prv_lin_none_kernel(tc, uT, wu, w_words, w_scales, gate, offs, out)
 
         def gated(e0, e1, bank_number):
             bank = experts(e0, e1, bank_number)
-            result = sbuf("result%d" % e0, [P, (e1 - e0) * C], F32)
-            nc.vector.tensor_tensor(result[:], bank[:], gates[:, e0 * C : e1 * C], MULT)
-            return result
+            nc.vector.tensor_tensor(by_slot[:, e0 * C : e1 * C], bank[:], gates[:, e0 * C : e1 * C], MULT)
 
-        def scatter_on_vector(e, values):
-            on_vector(windows[0][:].indirect(slot_offsets(e, e + 1)), values)
+        def scatter(copy, window, s0, s1):
+            copy(window[:].indirect(offsets[:, s0 // 16 : s1 // 16]), by_slot[:, s0:s1])
 
+        def scalar_scatter(target, source):
+            nc.scalar.activation(target, source, COPY)
+
+        by_slot = sbuf("by_slot", [P, T], F32)
         wu_bf = [sbuf("wu_bf%d" % g, [P, 4, P, 4], BF16) for g in range(G)]
         wu_codes = [sbuf("wu_codes%d" % g, [P, 4 * P], U32) for g in range(G)]
         wu_scales = [sbuf("wu_scales%d" % g, [P, 4 * P], U8) for g in range(G)]
@@ -174,38 +177,41 @@ def tile_moe_prv_lin_none_kernel(tc, uT, wu, w_words, w_scales, gate, offs, out)
         round_u(on_scalar, 0, 0, U_FIRST_ON_VECTOR, T)
         for i in range(3):
             round_u(on_scalar, 1, i, 0, 256)
-        for h in range(2):
-            gather(h, 0, 4)
-            gather(h, 4, 6)
+        gather(0, 0, 4)
+        gather(0, 4, 6)
+        gather(1, 0, 2)
+        gather(1, 2, 6)
         round_wu(on_scalar, 0, 0, 4)
         slots0 = weave(0, 0)
         slots2 = weave(2, raw_bytes // 2)
-        round_wu(on_vector, 1, 0, 2)
-        round_wu(on_vector, 1, 2, 4)
-        quantize_wu(0, 0, 2)
+        round_wu(on_vector, 1, 0, 4)
         quantize_u(slots0, 0)
+        quantize_wu(0, 0, 2)
         quantize_wu(0, 2, 4)
         quantize_u(slots2, 2)
         round_wu(on_scalar, 2, 0, 4)
         slots4 = weave(4, 2 * raw_bytes)
-        round_wu(on_vector, 3, 0, 2)
-        round_wu(on_vector, 3, 2, 4)
+        round_wu(on_vector, 3, 0, 3)
+        round_wu(on_scalar, 3, 3, 4)
+        quantize_u(slots4, 4)
         quantize_wu(1, 0, 2)
         quantize_wu(1, 2, 4)
-        quantize_u(slots4, 4)
 
-        make_x([(0, 0, 0, on_scalar), (1, 0, 1, on_scalar)])
-        make_x([(2, 0, 2, on_scalar), (3, 0, 3, on_vector)], overlaid("x_bf_20", [P, 8 * C], BF16, 3 * raw_bytes))
+        make_x([(0, 0, 0, on_scalar), (1, 0, 1, on_scalar)], overlaid("x_bf_00", [P, 8 * C], BF16, 3 * raw_bytes - raw_bytes // 2 + 64))
+        make_x([(2, 0, 2, on_scalar), (3, 0, 3, on_vector)], overlaid("x_bf_20", [P, 8 * C], BF16, 3 * raw_bytes + 64))
         make_x([(0, 1, 4, on_vector), (1, 1, 5, on_scalar)])
         make_x([(2, 1, 6, on_scalar), (3, 1, 7, on_scalar)])
-        first_results = gated(0, 4, 4)
-        make_x([(4, 0, 0, on_scalar), (4, 1, 1, on_scalar)], codes_tag="x_codes_21")
-        scatter_on_vector(3, first_results[:, 3 * C :])
-        fifth_result = gated(4, 5, 5)
-        make_x([(5, 0, 2, on_scalar), (5, 1, 3, on_scalar)], codes_tag="x_codes_21")
-        scatter_on_vector(4, fifth_result[:])
-        nc.scalar.activation(windows[1][:].indirect(slot_offsets(0, 3)), first_results[:, : 3 * C], COPY)
-        scatter_on_vector(5, gated(5, 6, 6)[:])
+        gated(0, 2, 4)
+        make_x([(4, 0, 0, on_scalar), (4, 1, 1, on_vector)], codes_tag="x_codes_01")
+        scatter(on_vector, windows[0], 0, FIRST_ON_VECTOR)
+        gated(2, 4, 5)
+        gated(4, 5, 6)
+        make_x([(5, 0, 2, on_scalar), (5, 1, 3, on_scalar)], codes_tag="x_codes_01")
+        scatter(on_vector, windows[0], 4 * C, 5 * C)
+        scatter(scalar_scatter, windows[1], FIRST_ON_VECTOR, 2 * C)
+        scatter(scalar_scatter, windows[1], 2 * C, 4 * C)
+        gated(5, 6, 7)
+        scatter(on_vector, windows[0], 5 * C, T)
         width = T // STORES
         for i in range(STORES):
             columns = slice(i * width, (i + 1) * width)

@@ -22,6 +22,7 @@ G = K // 512
 PIECE = 256
 U_FIRST_ON_VECTOR = 512
 FIRST_ON_VECTOR = 96
+WINDOW = 1024
 STORES = 3
 
 
@@ -43,7 +44,8 @@ def tile_moe_prv_lin_none_kernel(tc, uT, wu, w_words, w_scales, gate, offs, out)
         u_cuts = [[(0, T)], [(0, 256), (256, 512), (512, T)]]
         u_raw = [[sbuf("u_raw%d_%d" % (h, t0), [P, 2, t1 - t0], F32) for t0, t1 in u_cuts[h]] for h in range(2)]
         raw_bytes = 4 * PIECE * 4
-        wu_raw = [overlaid("wu_raw%d" % i, [P, 4, PIECE], F32, i * raw_bytes) for i in range(4)]
+        wu_cuts = [(0, 128), (128, 256), (256, 512), (512, 768), (768, K)]
+        wu_raw = [overlaid("wu_raw%d" % k0, [P, 4, k1 - k0], F32, i * raw_bytes) for i, (k0, k1) in enumerate(wu_cuts)]
         word_scales = sbuf("word_scales", [P, E * G, N], U8)
         gates = sbuf("gates", [P, T], F32)
         windows = [sbuf("window%d" % i, [P, T], F32) for i in range(2)]
@@ -59,8 +61,8 @@ def tile_moe_prv_lin_none_kernel(tc, uT, wu, w_words, w_scales, gate, offs, out)
                 nc.sync.dma_start(u_raw[h][i][:], u_rows[:, 2 * h : 2 * h + 2, t0:t1])
             if h == 0:
                 nc.sync.dma_start(offsets[:], offs)
-        for i in range(K // PIECE):
-            nc.sync.dma_start(wu_raw[i][:], wu_rows[:, :, PIECE * i : PIECE * (i + 1)])
+        for raw, (k0, k1) in zip(wu_raw, wu_cuts):
+            nc.sync.dma_start(raw[:], wu_rows[:, :, k0:k1])
         word_rows = w_words.rearrange("e a p n -> p (e a) n").bitcast(I32)
         words = sbuf("words", [P, E * G, 2 * N], U8)
         nc.sync.dma_start(gates[:], gate)
@@ -69,7 +71,8 @@ def tile_moe_prv_lin_none_kernel(tc, uT, wu, w_words, w_scales, gate, offs, out)
         for r in range(4):
             nc.sync.dma_start(word_scales[r:P:32].bitcast(I32), scale_rows[r])
 
-        pairs = [sbuf("pairs%d" % h, [P, 2 * T], BF16) for h in range(2)]
+        pairs = [sbuf("pairs0", [P, 2 * WINDOW], BF16), sbuf("pairs1", [P, 2 * T], BF16)]
+        nc.gpsimd.memset(pairs[0][:, 2 * T :], 0.0)
         planes = sbuf("planes", [P, 2 * T], U32)
         u_codes, u_scales = {}, {}
         x_bf, x_codes, x_scales = {}, {}, {}
@@ -85,9 +88,10 @@ def tile_moe_prv_lin_none_kernel(tc, uT, wu, w_words, w_scales, gate, offs, out)
             )
 
         def round_wu(copy, i, t0, t1):
-            m0 = 64 * (i % 2)
+            k0, k1 = wu_cuts[i]
+            m0, m1 = k0 % 512 // 4, (k1 - 1) % 512 // 4 + 1
             copy(
-                wu_bf[i // 2][:, t0:t1, m0 : m0 + 64, :].rearrange("p t m j -> p m t j"),
+                wu_bf[k0 // 512][:, t0:t1, m0:m1, :].rearrange("p t m j -> p m t j"),
                 wu_raw[i][:].rearrange("p j (m t) -> p m t j", t=4)[:, :, t0:t1, :],
             )
 
@@ -177,35 +181,35 @@ def tile_moe_prv_lin_none_kernel(tc, uT, wu, w_words, w_scales, gate, offs, out)
         round_u(on_scalar, 0, 0, U_FIRST_ON_VECTOR, T)
         for i in range(3):
             round_u(on_scalar, 1, i, 0, 256)
-        gather(0, 0, 4)
-        gather(0, 4, 6)
+        gather(0, 0, 6)
         gather(1, 0, 2)
-        gather(1, 2, 6)
+        gather(1, 2, 4)
+        gather(1, 4, 6)
         round_wu(on_scalar, 0, 0, 4)
+        round_wu(on_scalar, 1, 0, 4)
         slots0 = weave(0, 0)
-        slots2 = weave(2, raw_bytes // 2)
-        round_wu(on_vector, 1, 0, 4)
+        slots2 = weave(2, raw_bytes // 2 + 64)
+        slots4 = weave(4, raw_bytes + raw_bytes // 2 - 64)
+        round_wu(on_vector, 2, 0, 4)
         quantize_u(slots0, 0)
         quantize_wu(0, 0, 2)
         quantize_wu(0, 2, 4)
         quantize_u(slots2, 2)
-        round_wu(on_scalar, 2, 0, 4)
-        slots4 = weave(4, 2 * raw_bytes)
-        round_wu(on_vector, 3, 0, 3)
-        round_wu(on_scalar, 3, 3, 4)
         quantize_u(slots4, 4)
+        round_wu(on_scalar, 3, 0, 4)
+        round_wu(on_vector, 4, 0, 3)
+        round_wu(on_scalar, 4, 3, 4)
         quantize_wu(1, 0, 2)
         quantize_wu(1, 2, 4)
 
-        make_x([(0, 0, 0, on_scalar), (1, 0, 1, on_scalar)], overlaid("x_bf_00", [P, 8 * C], BF16, 3 * raw_bytes - raw_bytes // 2 + 64))
-        make_x([(2, 0, 2, on_scalar), (3, 0, 3, on_vector)], overlaid("x_bf_20", [P, 8 * C], BF16, 3 * raw_bytes + 64))
+        first_halves = [(0, 0, 0, on_scalar), (1, 0, 1, on_scalar), (2, 0, 2, on_scalar), (3, 0, 3, on_vector)]
+        make_x(first_halves, overlaid("x_bf_00", [P, 16 * C], BF16, 4 * raw_bytes))
         make_x([(0, 1, 4, on_vector), (1, 1, 5, on_scalar)])
         make_x([(2, 1, 6, on_scalar), (3, 1, 7, on_scalar)])
         gated(0, 2, 4)
         make_x([(4, 0, 0, on_scalar), (4, 1, 1, on_vector)], codes_tag="x_codes_01")
         scatter(on_vector, windows[0], 0, FIRST_ON_VECTOR)
-        gated(2, 4, 5)
-        gated(4, 5, 6)
+        gated(2, 5, 5)
         make_x([(5, 0, 2, on_scalar), (5, 1, 3, on_scalar)], codes_tag="x_codes_01")
         scatter(on_vector, windows[0], 4 * C, 5 * C)
         scatter(scalar_scatter, windows[1], FIRST_ON_VECTOR, 2 * C)

@@ -91,8 +91,8 @@ def tile_moe_prv_lin_none_kernel(tc, uT, wu, w_words, w_scales, gate, offs, out)
             k0, k1 = wu_cuts[i]
             m0, m1 = k0 % 512 // 4, (k1 - 1) % 512 // 4 + 1
             copy(
-                wu_bf[k0 // 512][:, t0:t1, m0:m1, :].rearrange("p t m j -> p m t j"),
-                wu_raw[i][:].rearrange("p j (m t) -> p m t j", t=4)[:, :, t0:t1, :],
+                wu_bf[k0 // 512][:, t0:t1, m0:m1, :].rearrange("p t m j -> p m j t"),
+                wu_raw[i][:].rearrange("p j (m t) -> p m j t", t=4)[:, :, :, t0:t1],
             )
 
         def quantize(codes, scales, values):
@@ -202,7 +202,7 @@ def tile_moe_prv_lin_none_kernel(tc, uT, wu, w_words, w_scales, gate, offs, out)
         quantize_wu(1, 0, 2)
         quantize_wu(1, 2, 4)
 
-        first_halves = [(0, 0, 0, on_scalar), (1, 0, 1, on_scalar), (2, 0, 2, on_scalar), (3, 0, 3, on_vector)]
+        first_halves = [(0, 0, 0, on_scalar), (1, 0, 1, on_vector), (2, 0, 2, on_scalar), (3, 0, 3, on_scalar)]
         make_x(first_halves, overlaid("x_bf_00", [P, 16 * C], BF16, 4 * raw_bytes))
         make_x([(0, 1, 4, on_vector), (1, 1, 5, on_scalar)])
         make_x([(2, 1, 6, on_scalar), (3, 1, 7, on_scalar)])

from contextlib import ExitStack

import concourse.mybir as mybir

K, T, E, C, N, M = 1024, 768, 6, 128, 128, 512
FLOPS = 2 * M * K * T + 2 * K * N * T

F32 = mybir.dt.float32
BF16 = mybir.dt.bfloat16
I32 = mybir.dt.int32
U32 = mybir.dt.uint32
U16 = mybir.dt.uint16
U8 = mybir.dt.uint8
FP8X4 = mybir.dt.float8_e4m3fn_x4
FP4X4 = mybir.dt.float4_e2m1fn_x4
MULT = mybir.AluOpType.mult
ADD = mybir.AluOpType.add
COPY = mybir.ActivationFunctionType.Copy

P = 128
G = K // 512
PIECE = 256
U_FIRST_ON_VECTOR = 512
FIRST_ON_VECTOR = 96
WINDOW = 1024
STORES = 3


def tile_moe_prv_lin_none_kernel(tc, uT, wu, w_words, w_scales, gate, offs, out):
    nc = tc.nc
    on_vector, on_scalar = nc.vector.tensor_copy, nc.scalar.copy
    with ExitStack() as ctx:
        keep = ctx.enter_context(tc.tile_pool(name="keep", bufs=1))
        shared = ctx.enter_context(tc.tile_pool(name="shared", bufs=1))
        psum = ctx.enter_context(tc.psum_pool(name="psum", bufs=1))

        def sbuf(name, shape, dtype, tag=None):
            return keep.tile(shape, dtype, name=name, tag=tag or name, align_bytes=64)

        def overlaid(name, shape, dtype, start):
            return shared.tile(shape, dtype, name=name, align_bytes=64, offset=start)

        offsets = keep.tile([P, T // 16], U16, name="offsets")
        u_cuts = [[(0, T)], [(0, 256), (256, 512), (512, T)]]
        u_raw = [[sbuf("u_raw%d_%d" % (h, t0), [P, 2, t1 - t0], F32) for t0, t1 in u_cuts[h]] for h in range(2)]
        raw_bytes = 4 * PIECE * 4
        wu_cuts = [(0, 128), (128, 256), (256, 512), (512, 768), (768, K)]
        wu_raw = [overlaid("wu_raw%d" % k0, [P, 4, k1 - k0], F32, i * raw_bytes) for i, (k0, k1) in enumerate(wu_cuts)]
        word_scales = sbuf("word_scales", [P, E * G, N], U8)
        gates = sbuf("gates", [P, T], F32)
        windows = [sbuf("window%d" % i, [P, T], F32) for i in range(2)]

        nc.gpsimd.memset(word_scales[:].bitcast(I32), 0)
        for window in windows:
            nc.gpsimd.memset(window[:], 0.0)

        u_rows = uT.rearrange("(p j) t -> p j t", j=4)
        wu_rows = wu.rearrange("(p j) k -> p j k", j=4)
        for h in range(2):
            for i, (t0, t1) in enumerate(u_cuts[h]):
                nc.sync.dma_start(u_raw[h][i][:], u_rows[:, 2 * h : 2 * h + 2, t0:t1])
            if h == 0:
                nc.sync.dma_start(offsets[:], offs)
        for raw, (k0, k1) in zip(wu_raw, wu_cuts):
            nc.sync.dma_start(raw[:], wu_rows[:, :, k0:k1])
        word_rows = w_words.rearrange("e a p n -> p (e a) n").bitcast(I32)
        words = sbuf("words", [P, E * G, 2 * N], U8)
        nc.sync.dma_start(gates[:], gate)
        nc.sync.dma_start(words[:].bitcast(I32), word_rows)
        scale_rows = w_scales.rearrange("e a (quad r) n -> r quad (e a) n", r=4).bitcast(I32)
        for r in range(4):
            nc.sync.dma_start(word_scales[r:P:32].bitcast(I32), scale_rows[r])

        pairs = [sbuf("pairs0", [P, 2 * WINDOW], BF16), sbuf("pairs1", [P, 2 * T], BF16)]
        nc.gpsimd.memset(pairs[0][:, 2 * T :], 0.0)
        planes = sbuf("planes", [P, 2 * T], U32)
        u_codes, u_scales = {}, {}
        x_bf, x_codes, x_scales = {}, {}, {}

        def slot_offsets(e0, e1):
            return offsets[:, e0 * C // 16 : e1 * C // 16]

        def round_u(copy, h, i, a, b):
            t0 = u_cuts[h][i][0]
            copy(
                pairs[h][:].rearrange("p (t e) -> p t e", e=2)[:, t0 + a : t0 + b, :],
                u_raw[h][i][:].rearrange("p e t -> p t e")[:, a:b, :],
            )

        def round_wu(copy, i, t0, t1):
            k0, k1 = wu_cuts[i]
            m0, m1 = k0 % 512 // 4, (k1 - 1) % 512 // 4 + 1
            copy(
                wu_bf[k0 // 512][:, t0:t1, m0:m1, :].rearrange("p t m j -> p m j t"),
                wu_raw[i][:].rearrange("p j (m t) -> p m j t", t=4)[:, :, :, t0:t1],
            )

        def quantize(codes, scales, values):
            nc.vector.quantize_mx(out=codes.bitcast(FP8X4), scales=scales, in_=values)

        def gather(h, e0, e1):
            on_vector(planes[:, h * T + e0 * C : h * T + e1 * C], pairs[h][:].bitcast(U32).indirect(slot_offsets(e0, e1)))

        def weave(e0, start):
            slots = overlaid("slots%d" % e0, [P, 8 * C], BF16, start)
            on_scalar(
                slots[:].bitcast(U32).rearrange("p (c h) -> p c h", h=2),
                planes[:].rearrange("p (h c) -> p c h", h=2)[:, e0 * C : (e0 + 2) * C, :],
            )
            return slots

        def quantize_u(slots, e0):
            codes = sbuf("u_codes%d" % e0, [P, 2 * C], U32)
            scales = sbuf("u_scales%d" % e0, [P, 2 * C], U8)
            for e in (e0, e0 + 1):
                u_codes[e] = codes[:, (e - e0) * C : (e - e0 + 1) * C]
                u_scales[e] = scales[:, (e - e0) * C : (e - e0 + 1) * C]
            quantize(codes[:], scales[:], slots[:])

        def quantize_wu(g, t0, t1):
            columns = slice(t0 * P, t1 * P)
            quantize(wu_codes[g][:, columns], wu_scales[g][:, columns], wu_bf[g][:, t0:t1].rearrange("p t m j -> p (t m j)"))

        def project(e, g, bank_number, copy, values):
            bank = psum.tile([P, 4, C], F32, name="bank", tag="bank%d" % bank_number)
            for t in range(4):
                nc.tensor.matmul_mx(
                    out=bank[:, t, :],
                    lhsT=wu_codes[g][:, t * P : (t + 1) * P].bitcast(FP8X4),
                    lhsT_scale=wu_scales[g][:, t * P : (t + 1) * P],
                    rhs=u_codes[e].bitcast(FP8X4),
                    rhs_scale=u_scales[e],
                    start=True,
                    stop=True,
                )
            copy(values.rearrange("p (c t) -> p c t", t=4), bank[:].rearrange("p t c -> p c t"))

        def make_x(halves, values=None, codes_tag=None):
            name = "_%d%d" % halves[0][:2]
            if values is None:
                values = sbuf("x_bf" + name, [P, len(halves) * 4 * C], BF16)
            codes = sbuf("x_codes" + name, [P, len(halves) * C], U32, codes_tag)
            scales = sbuf("x_scales" + name, [P, len(halves) * C], U8)
            for n, (e, g, bank_number, copy) in enumerate(halves):
                x_codes[e, g] = codes[:, n * C : (n + 1) * C]
                x_scales[e, g] = scales[:, n * C : (n + 1) * C]
                project(e, g, bank_number, copy, values[:, n * 4 * C : (n + 1) * 4 * C])
            quantize(codes[:], scales[:], values[:])

        def experts(e0, e1, bank_number):
            bank = psum.tile([P, (e1 - e0) * C], F32, name="bank", tag="bank%d" % bank_number)
            for e in range(e0, e1):
                for g in range(G):
                    nc.tensor.matmul_mx(
                        out=bank[:, (e - e0) * C : (e - e0 + 1) * C],
                        lhsT=words[:, e * G + g, :].bitcast(FP4X4),
                        lhsT_scale=word_scales[:, e * G + g, :],
                        rhs=x_codes[e, g].bitcast(FP8X4),
                        rhs_scale=x_scales[e, g],
                        start=(g == 0),
                        stop=(g == G - 1),
                    )
            return bank

        def gated(e0, e1, bank_number):
            bank = experts(e0, e1, bank_number)
            nc.vector.tensor_tensor(by_slot[:, e0 * C : e1 * C], bank[:], gates[:, e0 * C : e1 * C], MULT)

        def scatter(copy, window, s0, s1):
            copy(window[:].indirect(offsets[:, s0 // 16 : s1 // 16]), by_slot[:, s0:s1])

        def scalar_scatter(target, source):
            nc.scalar.activation(target, source, COPY)

        by_slot = sbuf("by_slot", [P, T], F32)
        wu_bf = [sbuf("wu_bf%d" % g, [P, 4, P, 4], BF16) for g in range(G)]
        wu_codes = [sbuf("wu_codes%d" % g, [P, 4 * P], U32) for g in range(G)]
        wu_scales = [sbuf("wu_scales%d" % g, [P, 4 * P], U8) for g in range(G)]

        round_u(on_vector, 0, 0, 0, U_FIRST_ON_VECTOR)
        round_u(on_scalar, 0, 0, U_FIRST_ON_VECTOR, T)
        for i in range(3):
            round_u(on_scalar, 1, i, 0, 256)
        gather(0, 0, 6)
        gather(1, 0, 2)
        gather(1, 2, 4)
        gather(1, 4, 6)
        round_wu(on_scalar, 0, 0, 4)
        round_wu(on_scalar, 1, 0, 4)
        slots0 = weave(0, 0)
        slots2 = weave(2, raw_bytes // 2 + 64)
        slots4 = weave(4, raw_bytes + raw_bytes // 2 - 64)
        round_wu(on_vector, 2, 0, 4)
        quantize_u(slots0, 0)
        quantize_wu(0, 0, 2)
        quantize_wu(0, 2, 4)
        quantize_u(slots2, 2)
        quantize_u(slots4, 4)
        round_wu(on_scalar, 3, 0, 4)
        round_wu(on_vector, 4, 0, 3)
        round_wu(on_scalar, 4, 3, 4)
        quantize_wu(1, 0, 2)
        quantize_wu(1, 2, 4)

        first_halves = [(0, 0, 0, on_scalar), (1, 0, 1, on_vector), (2, 0, 2, on_scalar), (3, 0, 3, on_scalar)]
        make_x(first_halves, overlaid("x_bf_00", [P, 16 * C], BF16, 4 * raw_bytes))
        make_x([(0, 1, 4, on_vector), (1, 1, 5, on_scalar)])
        make_x([(2, 1, 6, on_scalar), (3, 1, 7, on_scalar)])
        gated(0, 2, 4)
        make_x([(4, 0, 0, on_scalar), (4, 1, 1, on_vector)], codes_tag="x_codes_01")
        scatter(on_vector, windows[0], 0, FIRST_ON_VECTOR)
        gated(2, 5, 5)
        make_x([(5, 0, 2, on_scalar), (5, 1, 3, on_scalar)], codes_tag="x_codes_01")
        scatter(on_vector, windows[0], 4 * C, 5 * C)
        scatter(scalar_scatter, windows[1], FIRST_ON_VECTOR, 2 * C)
        scatter(scalar_scatter, windows[1], 2 * C, 4 * C)
        gated(5, 6, 7)
        scatter(on_vector, windows[0], 5 * C, T)
        width = T // STORES
        for i in range(STORES):
            columns = slice(i * width, (i + 1) * width)
            total = sbuf("total%d" % i, [P, width], F32)
            nc.vector.tensor_tensor(total[:], windows[0][:, columns], windows[1][:, columns], ADD)
            nc.sync.dma_start(out[:, columns], total[:])
